import numpy as np
import ml_dtypes


def mxq(x, axis, fmt="e4m3"):
    dtype, down = {"e4m3": (ml_dtypes.float8_e4m3fn, 7), "e5m2": (ml_dtypes.float8_e5m2, 14)}[fmt]
    v = np.moveaxis(np.asarray(x, np.float32).astype(ml_dtypes.bfloat16).astype(np.float64), axis, -1)
    blocks = v.reshape(v.shape[:-1] + (-1, 32))
    amax = np.abs(blocks).max(-1, keepdims=True)
    byte = np.maximum(np.where(amax > 0, np.frexp(amax)[1] - 1 + 127, 0) - down, 1)
    scale = np.exp2(byte - 127.0)
    codes = (blocks / scale).astype(np.float32).astype(dtype).astype(np.float64)
    return np.moveaxis((codes * scale).reshape(v.shape), -1, axis)


WIDE = False


def mx_kscale(k):
    if not WIDE:
        return np.ones(k)
    levels = np.array([24, -24, 12, -12, 0])
    if k % 512:
        return np.exp2(np.random.permutation(np.resize(levels, k // 32))).repeat(32)
    a = np.empty((k // 512, 16))
    for p in range(k // 512):
        a[p, :8] = np.random.permutation(np.resize(levels, 8))
        for g in range(8):
            far = levels[np.abs(levels - a[p, g]) >= 10]
            a[p, g + 8] = far[np.random.randint(len(far))]
    return np.exp2(a.ravel()).repeat(32)


def f64(x):
    return np.asarray(x).astype(np.float64)


def striped(idx):
    return np.tile(idx.reshape(-1, 16).T, (8, 1)).astype(np.uint16)


def unstriped(offs):
    return offs[:16].T.reshape(-1).astype(np.int64)


E2M1 = np.array([0.0, 0.5, 1.0, 1.5, 2.0, 3.0, 4.0, 6.0, -0.0, -0.5, -1.0, -1.5, -2.0, -3.0, -4.0, -6.0])


def pack_weight(w, fmt):
    k, n = w.shape
    w = f64(np.asarray(w, np.float32).astype(ml_dtypes.bfloat16)).reshape(k // 32, 32, n)
    amax = np.abs(w).max(1)
    if fmt == "e4m3":
        byte = np.frexp(amax)[1] - 1 + 127 - 7
    else:
        mant, ex = np.frexp(amax / 6.0)
        byte = np.where(mant > 0.5, ex, ex - 1) + 127
    byte = np.clip(np.where(amax > 0, byte, 1), 1, 254)
    scaled = (w * np.exp2(127.0 - byte)[:, None, :]).reshape(k, n).astype(np.float32)
    by_word = np.ascontiguousarray(scaled.reshape(k // 512, 128, 4, n).transpose(0, 1, 3, 2))
    if fmt == "e4m3":
        words = by_word.astype(ml_dtypes.float8_e4m3fn).view(np.uint8)
    else:
        c = by_word.astype(ml_dtypes.float4_e2m1fn).view(np.uint8) & 0xF
        words = (c[..., 0::2] | (c[..., 1::2] << 4)).reshape(k // 512, 128, 2 * n)
    return np.ascontiguousarray(words), np.ascontiguousarray(byte.astype(np.uint8).reshape(k // 512, 16, n))


def unpack_weight(words, scales, fmt):
    g, _, n = scales.shape
    words = np.ascontiguousarray(words).reshape(g, 128, n, -1)
    if fmt == "e4m3":
        vals = words.view(ml_dtypes.float8_e4m3fn).astype(np.float64)
    else:
        nib = np.empty((g, 128, n, 4), np.uint8)
        nib[..., 0::2] = words & 0xF
        nib[..., 1::2] = words >> 4
        vals = E2M1[nib]
    vals = vals * np.repeat(np.exp2(scales.astype(np.float64) - 127.0), 8, axis=1)[..., None]
    return vals.transpose(0, 1, 3, 2).reshape(g * 512, n)


def pack_table4(v):
    words, scales = pack_weight(v, "e2m1")
    g, t = words.shape[0] // 2, v.shape[1]
    return np.ascontiguousarray(words.reshape(g, 2, 128, t, 2).transpose(0, 2, 3, 1, 4).reshape(g, 128, t, 4)), scales


def unpack_table4(words, scales):
    g, _, t, _ = words.shape
    return unpack_weight(words.reshape(g, 128, t, 2, 2).transpose(0, 3, 1, 2, 4).reshape(2 * g, 128, 2 * t), scales, "e2m1")


K, L, N, T, J = 1024, 1024, 512, 4096, 512


def setup_inputs():
    n = np.random.standard_normal
    s = mx_kscale(K)[:, None]
    s2 = mx_kscale(L)[:, None]
    p_tab = pack_table4(n((K, T)) * s)
    p_wx = pack_weight(n((L, N)) / np.sqrt(L) / s2, "e4m3")
    return {
        "tab_words": p_tab[0],
        "tab_scales": p_tab[1],
        "w": (n((K, N)) / np.sqrt(K) / s).astype(np.float32),
        "x": (n((L, J)) * s2).astype(np.float32),
        "wx_words": p_wx[0],
        "wx_scales": p_wx[1],
        "iw0": (np.random.uniform(0.1, 0.6, J)).astype(np.float32),
        "iw1": (np.random.uniform(0.1, 0.6, J)).astype(np.float32),
        "iw2": (np.random.uniform(0.1, 0.6, J)).astype(np.float32),
        "offs": striped(np.concatenate([np.random.permutation(T)[:J] for _ in range(3)])),
    }


def reference(tab_words, tab_scales, w, x, wx_words, wx_scales, iw0, iw1, iw2, offs):
    idx = unstriped(offs).reshape(3, J)
    tab_ = unpack_table4(tab_words, tab_scales)[:, idx]
    w_ = mxq(f64(w), 0, "e4m3")
    a0 = w_.T @ tab_[:, 0]
    a1 = w_.T @ tab_[:, 1]
    a2 = w_.T @ tab_[:, 2]
    x_ = mxq(f64(x), 0, "e4m3")
    wx_ = unpack_weight(wx_words, wx_scales, "e4m3")
    ax = wx_.T @ x_
    return a0 * f64(iw0)[None, :] + a1 * f64(iw1)[None, :] + a2 * f64(iw2)[None, :] + ax

@@ -1,0 +1,221 @@
+from contextlib import ExitStack
+
+import concourse.mybir as mybir
+
+K, L, N, T, J = 1024, 1024, 512, 4096, 512
+G = 3
+FLOPS = 2 * (G * K + L) * N * J
+
+F32 = mybir.dt.float32
+BF16 = mybir.dt.bfloat16
+I32 = mybir.dt.int32
+U32 = mybir.dt.uint32
+U16 = mybir.dt.uint16
+U8 = mybir.dt.uint8
+FP8X4 = mybir.dt.float8_e4m3fn_x4
+FP4X4 = mybir.dt.float4_e2m1fn_x4
+COPY = mybir.ActivationFunctionType.Copy
+MULT = mybir.AluOpType.mult
+ADD = mybir.AluOpType.add
+EQUAL = mybir.AluOpType.is_equal
+
+P = 128
+PACK = 4
+K_PASS = P * PACK
+PASSES = 2
+TILES = 4
+SHIFT = 16
+
+
+def tile_list_interp_none_kernel(
+    tc, tab_words, tab_scales, w, x, wx_words, wx_scales, iw0, iw1, iw2, offs, out
+):
+    nc = tc.nc
+    with ExitStack() as ctx:
+        lists = ctx.enter_context(tc.tile_pool(name="lists", bufs=1))
+        keep = ctx.enter_context(tc.tile_pool(name="keep", bufs=1))
+        psum = ctx.enter_context(tc.psum_pool(name="psum", bufs=8))
+
+        tab_sc = keep.tile([P, T // 4], I32, name="tab_sc", align_bytes=64)
+        nc.vector.memset(tab_sc[:], 0)
+        iw_rows = keep.tile([P, P], F32, name="iw_rows")
+        nc.vector.memset(iw_rows[:], 0.0)
+        wx_sc = keep.tile([P, PASSES, N // 4], I32, name="wx_sc", align_bytes=64)
+        nc.vector.memset(wx_sc[:], 0)
+        sc_hi = keep.tile([P, G * J // 4], I32, name="sc_hi", align_bytes=64)
+        nc.vector.memset(sc_hi[:], 0)
+
+        tab_sc_hbm = tab_scales.bitcast(I32).rearrange("a (q r) t -> r q a t", r=4)
+        for r in range(4):
+            nc.gpsimd.dma_start(out=tab_sc[r:P:SHIFT, :], in_=tab_sc_hbm[r])
+        for g, vec in enumerate((iw0, iw1, iw2)):
+            nc.gpsimd.dma_start(
+                out=iw_rows[TILES * g : TILES * (g + 1), :],
+                in_=vec.rearrange("(c p) -> c p", p=P),
+            )
+        wx_sc_hbm = wx_scales.bitcast(I32).rearrange("a (q r) n -> r q a n", r=4)
+        for r in range(4):
+            nc.gpsimd.dma_start(out=wx_sc[r:P:32, :, :], in_=wx_sc_hbm[r])
+
+        def load_pass(src, a, name):
+            raw = keep.tile([P, PACK, 512], F32, name=name)
+            nc.sync.dma_start(
+                out=raw[:],
+                in_=src[a * K_PASS : (a + 1) * K_PASS, :].rearrange("(p i) c -> p i c", i=PACK),
+            )
+            return raw
+
+        w_raw = [load_pass(w, 0, "w_raw0")]
+        offsets = lists.tile([P, G * J // 16], U16, name="offsets")
+        nc.sync.dma_start(offsets[:], offs)
+        tab_w = keep.tile([P, T], I32, name="tab_w", align_bytes=64)
+        nc.sync.dma_start(
+            out=tab_w[:], in_=tab_words[0].rearrange("p t b -> p (t b)").bitcast(I32)
+        )
+        w_raw.append(load_pass(w, 1, "w_raw1"))
+        x_raw = [load_pass(x, a, f"x_raw{a}") for a in range(PASSES)]
+        wx_w = keep.tile([P, PASSES, N], I32, name="wx_w", align_bytes=64)
+        nc.sync.dma_start(
+            out=wx_w[:], in_=wx_words.rearrange("a p n b -> p a (n b)").bitcast(I32)
+        )
+
+        ones = keep.tile([P, P], F32, name="ones")
+        nc.vector.memset(ones[:], 1.0)
+        ident = keep.tile([P, P], F32, name="ident")
+        nc.vector.memset(ident[:], 0.0)
+        ramp = keep.tile([P, P], F32, name="ramp", align_bytes=64)
+        nc.vector.tensor_tensor_scan(
+            out=ramp[:], data0=ones[:], data1=ones[:], initial=0.0, op0=MULT, op1=ADD
+        )
+        ramp_turned = keep.tile([P, P], F32, name="ramp_turned", align_bytes=64)
+        nc.vector.transpose(ramp_turned[:], ramp[:])
+        for q in range(4):
+            blk = slice(32 * q, 32 * (q + 1))
+            nc.vector.tensor_tensor(
+                out=ident[blk, blk], in0=ramp[blk, blk], in1=ramp_turned[blk, blk], op=EQUAL
+            )
+
+        iw_turned = psum.tile([P, P], F32, name="bank")
+        nc.tensor.transpose(iw_turned[:], iw_rows[:], ident[:])
+        iw_cols = keep.tile([P, G, TILES], F32, name="iw_cols")
+        nc.scalar.copy(
+            out=iw_cols[:].rearrange("p g c -> p (g c)"), in_=iw_turned[:, 0 : G * TILES]
+        )
+
+        def cast(raw, name, on_vector):
+            grouped = keep.tile([P, 512, PACK], BF16, name=name, align_bytes=64)
+            cut = 512 - on_vector
+            if cut > 0:
+                nc.scalar.activation(
+                    out=grouped[:, 0:cut, :].rearrange("p (c u) i -> p c i u", u=4),
+                    in_=raw[:, :, 0:cut].rearrange("p i (c u) -> p c i u", u=4),
+                    func=COPY,
+                )
+            if on_vector > 0:
+                nc.vector.tensor_copy(
+                    out=grouped[:, cut:512, :].rearrange("p (c u) i -> p c i u", u=4),
+                    in_=raw[:, :, cut:512].rearrange("p i (c u) -> p c i u", u=4),
+                )
+            return grouped
+
+        def quantize(grouped, name):
+            codes = keep.tile([P, 512], U32, name=name + "_codes", align_bytes=64)
+            scales = keep.tile([P, 512], U8, name=name + "_scales", align_bytes=64)
+            nc.vector.quantize_mx(
+                out=codes[:].bitcast(FP8X4),
+                scales=scales[:],
+                in_=grouped[:].rearrange("p c i -> p (c i)"),
+            )
+            return codes, scales
+
+        sc_lo = keep.tile([P, G * J], U8, name="sc_lo", align_bytes=64)
+        nc.vector.tensor_copy(sc_lo[:], tab_sc[:].bitcast(U8).indirect(offsets[:]))
+        w_bf0 = cast(w_raw[0], "w_bf0", 0)
+        nc.scalar.dma_start(
+            out=sc_hi[0 : P - SHIFT, :], in_=sc_lo[SHIFT:P, :].bitcast(I32)
+        )
+        wq = [quantize(w_bf0, "wq0")]
+        tab_planes = [sc_lo[:], sc_hi[:].bitcast(U8)]
+
+        parted = []
+        for g in range(G):
+            both = keep.tile([P, J], U32, name=f"both{g}", align_bytes=64)
+            nc.vector.tensor_copy(
+                both[:],
+                tab_w[:].bitcast(U32).indirect(offsets[:, g * (J // 16) : (g + 1) * (J // 16)]),
+            )
+            apart = keep.tile([P, PASSES, 2 * J], U8, name=f"apart{g}", align_bytes=64)
+            nc.vector.tensor_copy(
+                out=apart[:].bitcast(U16),
+                in_=both[:].bitcast(U16).rearrange("p (j d) -> p d j", d=PASSES),
+            )
+            parted.append(apart)
+            if g == 0:
+                wq.append(quantize(cast(w_raw[1], "w_bf1", 0), "wq1"))
+
+        xq = [quantize(cast(x_raw[a], f"x_bf{a}", (0, 512)[a]), f"xq{a}") for a in range(PASSES)]
+
+        part = [None] * TILES
+
+        def interpolate(g):
+            for jt in range(TILES):
+                acc = psum.tile([P, N], F32, name="bank")
+                for a in range(PASSES):
+                    nc.tensor.matmul_mx(
+                        out=acc[:],
+                        lhsT=parted[g][:, a, 2 * P * jt : 2 * P * (jt + 1)].bitcast(FP4X4),
+                        lhsT_scale=tab_planes[a][:, g * J + P * jt : g * J + P * (jt + 1)],
+                        rhs=wq[a][0][:].bitcast(FP8X4),
+                        rhs_scale=wq[a][1][:],
+                        start=(a == 0),
+                        stop=(a == PASSES - 1),
+                    )
+                nxt = keep.tile([P, N], F32, name=f"part{g}_{jt}")
+                if g == 0:
+                    nc.scalar.activation(
+                        out=nxt[:], in_=acc[:], func=COPY, scale=iw_cols[:, g, jt : jt + 1]
+                    )
+                else:
+                    nc.vector.scalar_tensor_tensor(
+                        out=nxt[:],
+                        in0=acc[:],
+                        scalar=iw_cols[:, g, jt : jt + 1],
+                        in1=part[jt][:],
+                        op0=MULT,
+                        op1=ADD,
+                    )
+                part[jt] = nxt
+
+        dense = keep.tile([P, TILES, J], F32, name="dense")
+        wx_planes = wx_sc[:].bitcast(U8)
+
+        def project_x():
+            for nt in range(TILES):
+                acc = psum.tile([P, J], F32, name="bank")
+                for a in range(PASSES):
+                    nc.tensor.matmul_mx(
+                        out=acc[:],
+                        lhsT=wx_w[:, a, P * nt : P * (nt + 1)].bitcast(FP8X4),
+                        lhsT_scale=wx_planes[:, a, P * nt : P * (nt + 1)],
+                        rhs=xq[a][0][:].bitcast(FP8X4),
+                        rhs_scale=xq[a][1][:],
+                        start=(a == 0),
+                        stop=(a == PASSES - 1),
+                    )
+                nc.scalar.copy(out=dense[:, nt, :], in_=acc[:])
+
+        for g in range(G):
+            interpolate(g)
+        project_x()
+
+        out_tiles = out.rearrange("(nt p) j -> p nt j", p=P)
+        for jt in range(TILES):
+            cols = slice(P * jt, P * (jt + 1))
+            turned = psum.tile([P, TILES, P], F32, name="bank")
+            for nt in range(TILES):
+                nc.tensor.transpose(
+                    turned[:, nt, :], part[jt][:, P * nt : P * (nt + 1)], ident[:]
+                )
+            res = keep.tile([P, TILES, P], F32, name=f"res{jt}")
+            nc.vector.tensor_tensor(out=res[:], in0=turned[:], in1=dense[:, :, cols], op=ADD)
+            nc.sync.dma_start(out=out_tiles[:, :, cols], in_=res[:])

@@ -20,11 +20,19 @@ ADD = mybir.AluOpType.add
 EQUAL = mybir.AluOpType.is_equal
 
 P = 128
+QUAD = 32
+QUADS = P // QUAD
 PACK = 4
 K_PASS = P * PACK
 PASSES = 2
+WIDTH = 512
 TILES = 4
-SHIFT = 16
+ROWS_A_QUAD = 4
+SPREAD = 4
+LIST_COLUMNS = J // 16
+PSUM_BANKS = 8
+X0_ON_VECTOR = 256
+DENSE_AHEAD = 2
 
 
 def tile_list_interp_none_kernel(
@@ -34,93 +42,100 @@ def tile_list_interp_none_kernel(
     with ExitStack() as ctx:
         lists = ctx.enter_context(tc.tile_pool(name="lists", bufs=1))
         keep = ctx.enter_context(tc.tile_pool(name="keep", bufs=1))
-        psum = ctx.enter_context(tc.psum_pool(name="psum", bufs=8))
+        psum = ctx.enter_context(tc.psum_pool(name="psum", bufs=PSUM_BANKS))
 
-        tab_sc = keep.tile([P, T // 4], I32, name="tab_sc", align_bytes=64)
-        nc.vector.memset(tab_sc[:], 0)
-        iw_rows = keep.tile([P, P], F32, name="iw_rows")
-        nc.vector.memset(iw_rows[:], 0.0)
-        wx_sc = keep.tile([P, PASSES, N // 4], I32, name="wx_sc", align_bytes=64)
-        nc.vector.memset(wx_sc[:], 0)
-        sc_hi = keep.tile([P, G * J // 4], I32, name="sc_hi", align_bytes=64)
-        nc.vector.memset(sc_hi[:], 0)
-
-        tab_sc_hbm = tab_scales.bitcast(I32).rearrange("a (q r) t -> r q a t", r=4)
-        for r in range(4):
-            nc.gpsimd.dma_start(out=tab_sc[r:P:SHIFT, :], in_=tab_sc_hbm[r])
-        for g, vec in enumerate((iw0, iw1, iw2)):
-            nc.gpsimd.dma_start(
-                out=iw_rows[TILES * g : TILES * (g + 1), :],
-                in_=vec.rearrange("(c p) -> c p", p=P),
-            )
-        wx_sc_hbm = wx_scales.bitcast(I32).rearrange("a (q r) n -> r q a n", r=4)
-        for r in range(4):
-            nc.gpsimd.dma_start(out=wx_sc[r:P:32, :, :], in_=wx_sc_hbm[r])
+        scale_window = keep.tile(
+            [P, T // 4], I32, name="scale_window", tag="reused", align_bytes=64
+        )
+        nc.vector.memset(scale_window[:], 0)
+        ident = keep.tile([P, P], F32, name="ident")
+        nc.vector.memset(ident[:], 0.0)
+        iw_rows = keep.tile([P, P], F32, name="iw_rows", align_bytes=64)
+        nc.scalar.activation(out=iw_rows[:], in_=ident[:], func=COPY)
+        wx_scale = keep.tile([P, PASSES, N // 4], I32, name="wx_scale", align_bytes=64)
+        nc.vector.memset(wx_scale[:], 0)
+        tab_scale = keep.tile([P, PASSES, G * J // 4], I32, name="tab_scale", align_bytes=64)
+        nc.vector.memset(tab_scale[:], 0)
 
         def load_pass(src, a, name):
-            raw = keep.tile([P, PACK, 512], F32, name=name)
-            nc.sync.dma_start(
-                out=raw[:],
-                in_=src[a * K_PASS : (a + 1) * K_PASS, :].rearrange("(p i) c -> p i c", i=PACK),
-            )
+            raw = keep.tile([P, PACK, WIDTH], F32, name=name)
+            rows = src[a * K_PASS : (a + 1) * K_PASS, :]
+            nc.sync.dma_start(out=raw[:], in_=rows.rearrange("(p i) c -> p i c", i=PACK))
             return raw
 
         w_raw = [load_pass(w, 0, "w_raw0")]
-        offsets = lists.tile([P, G * J // 16], U16, name="offsets")
+
+        offsets = lists.tile([P, G * LIST_COLUMNS], U16, name="offsets")
         nc.sync.dma_start(offsets[:], offs)
-        tab_w = keep.tile([P, T], I32, name="tab_w", align_bytes=64)
+
         nc.sync.dma_start(
-            out=tab_w[:], in_=tab_words[0].rearrange("p t b -> p (t b)").bitcast(I32)
+            out=scale_window[0:P:SPREAD, :],
+            in_=tab_scales.bitcast(I32).rearrange("a s t -> (a s) t"),
         )
+        word_window = keep.tile([P, T], I32, name="word_window", align_bytes=64)
+        nc.sync.dma_start(
+            out=word_window[:], in_=tab_words[0].rearrange("p t b -> p (t b)").bitcast(I32)
+        )
+        for g, vec in enumerate((iw0, iw1, iw2)):
+            nc.sync.dma_start(
+                out=iw_rows[g:P:QUAD, :].rearrange("q (c i) -> q c i", i=QUAD),
+                in_=vec.rearrange("(c q i) -> q c i", q=QUADS, i=QUAD),
+            )
         w_raw.append(load_pass(w, 1, "w_raw1"))
-        x_raw = [load_pass(x, a, f"x_raw{a}") for a in range(PASSES)]
-        wx_w = keep.tile([P, PASSES, N], I32, name="wx_w", align_bytes=64)
+
+        picked_scales = keep.tile([P, G * J], U8, name="picked_scales", align_bytes=64)
+        nc.vector.tensor_copy(picked_scales[:], scale_window[:].bitcast(U8).indirect(offsets[:]))
+
+        def place_scales(a):
+            first = a * QUADS * ROWS_A_QUAD * SPREAD
+            step = ROWS_A_QUAD * SPREAD
+            for r in range(ROWS_A_QUAD):
+                rows = slice(first + SPREAD * r, first + QUADS * step, step)
+                nc.sync.dma_start(
+                    out=tab_scale[r:P:QUAD, a, :], in_=picked_scales[rows, :].bitcast(I32)
+                )
+
+        place_scales(0)
+        x_raw = [load_pass(x, 0, "x_raw0")]
+        place_scales(1)
+        wx_word = keep.tile([P, PASSES, N], I32, name="wx_word", align_bytes=64)
         nc.sync.dma_start(
-            out=wx_w[:], in_=wx_words.rearrange("a p n b -> p a (n b)").bitcast(I32)
+            out=wx_word[:], in_=wx_words.rearrange("a p n b -> p a (n b)").bitcast(I32)
         )
+        x_raw.append(load_pass(x, 1, "x_raw1"))
+        wx_scale_rows = wx_scales.bitcast(I32).rearrange("a (q r) n -> r q a n", r=ROWS_A_QUAD)
+        for r in range(ROWS_A_QUAD):
+            nc.sync.dma_start(out=wx_scale[r:P:QUAD, :, :], in_=wx_scale_rows[r])
 
         ones = keep.tile([P, P], F32, name="ones")
         nc.vector.memset(ones[:], 1.0)
-        ident = keep.tile([P, P], F32, name="ident")
-        nc.vector.memset(ident[:], 0.0)
         ramp = keep.tile([P, P], F32, name="ramp", align_bytes=64)
         nc.vector.tensor_tensor_scan(
             out=ramp[:], data0=ones[:], data1=ones[:], initial=0.0, op0=MULT, op1=ADD
         )
         ramp_turned = keep.tile([P, P], F32, name="ramp_turned", align_bytes=64)
         nc.vector.transpose(ramp_turned[:], ramp[:])
-        for q in range(4):
-            blk = slice(32 * q, 32 * (q + 1))
+        for q in range(QUADS):
+            blk = slice(QUAD * q, QUAD * (q + 1))
             nc.vector.tensor_tensor(
                 out=ident[blk, blk], in0=ramp[blk, blk], in1=ramp_turned[blk, blk], op=EQUAL
             )
 
-        iw_turned = psum.tile([P, P], F32, name="bank")
-        nc.tensor.transpose(iw_turned[:], iw_rows[:], ident[:])
-        iw_cols = keep.tile([P, G, TILES], F32, name="iw_cols")
-        nc.scalar.copy(
-            out=iw_cols[:].rearrange("p g c -> p (g c)"), in_=iw_turned[:, 0 : G * TILES]
-        )
+        def quantize(raw, name, codes_tag, on_vector=0):
+            grouped = keep.tile([P, WIDTH, PACK], BF16, name=name + "_bf16", align_bytes=64)
 
-        def cast(raw, name, on_vector):
-            grouped = keep.tile([P, 512, PACK], BF16, name=name, align_bytes=64)
-            cut = 512 - on_vector
-            if cut > 0:
-                nc.scalar.activation(
-                    out=grouped[:, 0:cut, :].rearrange("p (c u) i -> p c i u", u=4),
-                    in_=raw[:, :, 0:cut].rearrange("p i (c u) -> p c i u", u=4),
-                    func=COPY,
-                )
-            if on_vector > 0:
-                nc.vector.tensor_copy(
-                    out=grouped[:, cut:512, :].rearrange("p (c u) i -> p c i u", u=4),
-                    in_=raw[:, :, cut:512].rearrange("p i (c u) -> p c i u", u=4),
-                )
-            return grouped
+            def sides(cols):
+                return {
+                    "out": grouped[:, cols, :].rearrange("p (c u) i -> p c i u", u=4),
+                    "in_": raw[:, :, cols].rearrange("p i (c u) -> p c i u", u=4),
+                }
 
-        def quantize(grouped, name):
-            codes = keep.tile([P, 512], U32, name=name + "_codes", align_bytes=64)
-            scales = keep.tile([P, 512], U8, name=name + "_scales", align_bytes=64)
+            cut = WIDTH - on_vector
+            nc.scalar.activation(func=COPY, **sides(slice(0, cut)))
+            if on_vector:
+                nc.vector.tensor_copy(**sides(slice(cut, WIDTH)))
+            codes = keep.tile([P, WIDTH], U32, name=name + "_codes", tag=codes_tag, align_bytes=64)
+            scales = keep.tile([P, WIDTH], U8, name=name + "_scales", align_bytes=64)
             nc.vector.quantize_mx(
                 out=codes[:].bitcast(FP8X4),
                 scales=scales[:],
@@ -128,94 +143,97 @@ def tile_list_interp_none_kernel(
             )
             return codes, scales
 
-        sc_lo = keep.tile([P, G * J], U8, name="sc_lo", align_bytes=64)
-        nc.vector.tensor_copy(sc_lo[:], tab_sc[:].bitcast(U8).indirect(offsets[:]))
-        w_bf0 = cast(w_raw[0], "w_bf0", 0)
-        nc.scalar.dma_start(
-            out=sc_hi[0 : P - SHIFT, :], in_=sc_lo[SHIFT:P, :].bitcast(I32)
-        )
-        wq = [quantize(w_bf0, "wq0")]
-        tab_planes = [sc_lo[:], sc_hi[:].bitcast(U8)]
-
-        parted = []
-        for g in range(G):
+        def look_up(g):
             both = keep.tile([P, J], U32, name=f"both{g}", align_bytes=64)
-            nc.vector.tensor_copy(
-                both[:],
-                tab_w[:].bitcast(U32).indirect(offsets[:, g * (J // 16) : (g + 1) * (J // 16)]),
-            )
+            entries = offsets[:, g * LIST_COLUMNS : (g + 1) * LIST_COLUMNS]
+            nc.vector.tensor_copy(both[:], word_window[:].bitcast(U32).indirect(entries))
             apart = keep.tile([P, PASSES, 2 * J], U8, name=f"apart{g}", align_bytes=64)
             nc.vector.tensor_copy(
                 out=apart[:].bitcast(U16),
-                in_=both[:].bitcast(U16).rearrange("p (j d) -> p d j", d=PASSES),
+                in_=both[:].bitcast(U16).rearrange("p (j a) -> p a j", a=PASSES),
             )
-            parted.append(apart)
+            return apart
+
+        wq = [quantize(w_raw[0], "w0", "reused")]
+        picked = [look_up(g) for g in range(G)]
+        wq.append(quantize(w_raw[1], "w1", "w1_codes"))
+        iw_cols = keep.tile([P, P], F32, name="iw_cols", align_bytes=64)
+        nc.vector.transpose(iw_cols[:], iw_rows[:])
+        xq = [
+            quantize(x_raw[0], "x0", "x0_codes", X0_ON_VECTOR),
+            quantize(x_raw[1], "x1", "x1_codes"),
+        ]
+
+        tab_scale_bytes = tab_scale[:].bitcast(U8)
+        partial = [None] * TILES
+
+        def add_look_up(g, jt):
+            acc = psum.tile([P, N], F32, name="bank")
+            for a in range(PASSES):
+                nc.tensor.matmul_mx(
+                    out=acc[:],
+                    lhsT=picked[g][:, a, 2 * P * jt : 2 * P * (jt + 1)].bitcast(FP4X4),
+                    lhsT_scale=tab_scale_bytes[:, a, g * J + P * jt : g * J + P * (jt + 1)],
+                    rhs=wq[a][0][:].bitcast(FP8X4),
+                    rhs_scale=wq[a][1][:],
+                    start=(a == 0),
+                    stop=(a == PASSES - 1),
+                )
+            weight = iw_cols[:, QUAD * jt + g : QUAD * jt + g + 1]
+            total = keep.tile([P, N], F32, name=f"partial{g}_{jt}")
             if g == 0:
-                wq.append(quantize(cast(w_raw[1], "w_bf1", 0), "wq1"))
+                nc.scalar.activation(out=total[:], in_=acc[:], func=COPY, scale=weight)
+            else:
+                nc.vector.scalar_tensor_tensor(
+                    out=total[:], in0=acc[:], scalar=weight, in1=partial[jt][:], op0=MULT, op1=ADD
+                )
+            partial[jt] = total
 
-        xq = [quantize(cast(x_raw[a], f"x_bf{a}", (0, 512)[a]), f"xq{a}") for a in range(PASSES)]
+        steps = [(g, half) for g in range(G) for half in range(2)]
+        for g, half in sorted(steps, key=lambda s: 2 * s[0] + 3 * s[1]):
+            for jt in (2 * half, 2 * half + 1):
+                add_look_up(g, jt)
 
-        part = [None] * TILES
+        wx_scale_bytes = wx_scale[:].bitcast(U8)
 
-        def interpolate(g):
-            for jt in range(TILES):
-                acc = psum.tile([P, N], F32, name="bank")
-                for a in range(PASSES):
-                    nc.tensor.matmul_mx(
-                        out=acc[:],
-                        lhsT=parted[g][:, a, 2 * P * jt : 2 * P * (jt + 1)].bitcast(FP4X4),
-                        lhsT_scale=tab_planes[a][:, g * J + P * jt : g * J + P * (jt + 1)],
-                        rhs=wq[a][0][:].bitcast(FP8X4),
-                        rhs_scale=wq[a][1][:],
-                        start=(a == 0),
-                        stop=(a == PASSES - 1),
-                    )
-                nxt = keep.tile([P, N], F32, name=f"part{g}_{jt}")
-                if g == 0:
-                    nc.scalar.activation(
-                        out=nxt[:], in_=acc[:], func=COPY, scale=iw_cols[:, g, jt : jt + 1]
-                    )
-                else:
-                    nc.vector.scalar_tensor_tensor(
-                        out=nxt[:],
-                        in0=acc[:],
-                        scalar=iw_cols[:, g, jt : jt + 1],
-                        in1=part[jt][:],
-                        op0=MULT,
-                        op1=ADD,
-                    )
-                part[jt] = nxt
+        def dense_pass(acc, nt, a):
+            nc.tensor.matmul_mx(
+                out=acc[:],
+                lhsT=wx_word[:, a, P * nt : P * (nt + 1)].bitcast(FP8X4),
+                lhsT_scale=wx_scale_bytes[:, a, P * nt : P * (nt + 1)],
+                rhs=xq[a][0][:].bitcast(FP8X4),
+                rhs_scale=xq[a][1][:],
+                start=(a == 0),
+                stop=(a == PASSES - 1),
+            )
 
-        dense = keep.tile([P, TILES, J], F32, name="dense")
-        wx_planes = wx_sc[:].bitcast(U8)
+        dense = []
+        for nt in range(DENSE_AHEAD):
+            acc = psum.tile([P, J], F32, name="bank")
+            dense_pass(acc, nt, 0)
+            dense.append(acc)
 
-        def project_x():
-            for nt in range(TILES):
-                acc = psum.tile([P, J], F32, name="bank")
-                for a in range(PASSES):
-                    nc.tensor.matmul_mx(
-                        out=acc[:],
-                        lhsT=wx_w[:, a, P * nt : P * (nt + 1)].bitcast(FP8X4),
-                        lhsT_scale=wx_planes[:, a, P * nt : P * (nt + 1)],
-                        rhs=xq[a][0][:].bitcast(FP8X4),
-                        rhs_scale=xq[a][1][:],
-                        start=(a == 0),
-                        stop=(a == PASSES - 1),
-                    )
-                nc.scalar.copy(out=dense[:, nt, :], in_=acc[:])
-
-        for g in range(G):
-            interpolate(g)
-        project_x()
-
-        out_tiles = out.rearrange("(nt p) j -> p nt j", p=P)
+        turned = [psum.tile([P, J], F32, name="bank") for nt in range(TILES)]
         for jt in range(TILES):
-            cols = slice(P * jt, P * (jt + 1))
-            turned = psum.tile([P, TILES, P], F32, name="bank")
             for nt in range(TILES):
                 nc.tensor.transpose(
-                    turned[:, nt, :], part[jt][:, P * nt : P * (nt + 1)], ident[:]
+                    turned[nt][:, P * jt : P * (jt + 1)],
+                    partial[jt][:, P * nt : P * (nt + 1)],
+                    ident[:],
                 )
-            res = keep.tile([P, TILES, P], F32, name=f"res{jt}")
-            nc.vector.tensor_tensor(out=res[:], in0=turned[:], in1=dense[:, :, cols], op=ADD)
-            nc.sync.dma_start(out=out_tiles[:, :, cols], in_=res[:])
+        interpolated = keep.tile([P, TILES, J], F32, name="interpolated")
+        for nt in range(TILES):
+            nc.scalar.copy(out=interpolated[:, nt, :], in_=turned[nt][:])
+
+        for nt in range(TILES):
+            if nt >= DENSE_AHEAD:
+                acc = psum.tile([P, J], F32, name="bank")
+                dense_pass(acc, nt, 0)
+                dense.append(acc)
+            dense_pass(dense[nt], nt, 1)
+        for nt in range(TILES):
+            result = keep.tile([P, J], F32, name=f"result{nt}")
+            nc.vector.tensor_tensor(
+                out=result[:], in0=dense[nt][:], in1=interpolated[:, nt, :], op=ADD
+            )
+            nc.sync.dma_start(out=out[P * nt : P * (nt + 1), :], in_=result[:])

@@ -31,8 +31,9 @@ ROWS_A_QUAD = 4
 SPREAD = 4
 LIST_COLUMNS = J // 16
 PSUM_BANKS = 8
-X0_ON_VECTOR = 256
-DENSE_AHEAD = 2
+WARM_UP_PASSES = 3
+HALVES = 2
+HALF = WIDTH // HALVES
 
 
 def tile_list_interp_none_kernel(
@@ -42,7 +43,7 @@ def tile_list_interp_none_kernel(
     with ExitStack() as ctx:
         lists = ctx.enter_context(tc.tile_pool(name="lists", bufs=1))
         keep = ctx.enter_context(tc.tile_pool(name="keep", bufs=1))
-        psum = ctx.enter_context(tc.psum_pool(name="psum", bufs=PSUM_BANKS))
+        psum = ctx.enter_context(tc.psum_pool(name="psum", bufs=1))
 
         scale_window = keep.tile(
             [P, T // 4], I32, name="scale_window", tag="reused", align_bytes=64
@@ -78,8 +79,8 @@ def tile_list_interp_none_kernel(
         )
         for g, vec in enumerate((iw0, iw1, iw2)):
             nc.sync.dma_start(
-                out=iw_rows[g:P:QUAD, :].rearrange("q (c i) -> q c i", i=QUAD),
-                in_=vec.rearrange("(c q i) -> q c i", q=QUADS, i=QUAD),
+                out=iw_rows[TILES * g : TILES * (g + 1), :],
+                in_=vec.rearrange("(c p) -> c p", p=P),
             )
         w_raw.append(load_pass(w, 1, "w_raw1"))
 
@@ -98,11 +99,11 @@ def tile_list_interp_none_kernel(
         place_scales(0)
         x_raw = [load_pass(x, 0, "x_raw0")]
         place_scales(1)
+        x_raw.append(load_pass(x, 1, "x_raw1"))
         wx_word = keep.tile([P, PASSES, N], I32, name="wx_word", align_bytes=64)
         nc.sync.dma_start(
             out=wx_word[:], in_=wx_words.rearrange("a p n b -> p a (n b)").bitcast(I32)
         )
-        x_raw.append(load_pass(x, 1, "x_raw1"))
         wx_scale_rows = wx_scales.bitcast(I32).rearrange("a (q r) n -> r q a n", r=ROWS_A_QUAD)
         for r in range(ROWS_A_QUAD):
             nc.sync.dma_start(out=wx_scale[r:P:QUAD, :, :], in_=wx_scale_rows[r])
@@ -121,66 +122,97 @@ def tile_list_interp_none_kernel(
                 out=ident[blk, blk], in0=ramp[blk, blk], in1=ramp_turned[blk, blk], op=EQUAL
             )
 
-        def quantize(raw, name, codes_tag, on_vector=0):
-            grouped = keep.tile([P, WIDTH, PACK], BF16, name=name + "_bf16", align_bytes=64)
-
-            def sides(cols):
-                return {
-                    "out": grouped[:, cols, :].rearrange("p (c u) i -> p c i u", u=4),
-                    "in_": raw[:, :, cols].rearrange("p i (c u) -> p c i u", u=4),
-                }
-
-            cut = WIDTH - on_vector
-            nc.scalar.activation(func=COPY, **sides(slice(0, cut)))
+        def cast(grouped, raw, on_vector=False):
+            target = grouped.rearrange("p (c u) i -> p c i u", u=4)
+            source = raw.rearrange("p i (c u) -> p c i u", u=4)
             if on_vector:
-                nc.vector.tensor_copy(**sides(slice(cut, WIDTH)))
-            codes = keep.tile([P, WIDTH], U32, name=name + "_codes", tag=codes_tag, align_bytes=64)
-            scales = keep.tile([P, WIDTH], U8, name=name + "_scales", align_bytes=64)
-            nc.vector.quantize_mx(
-                out=codes[:].bitcast(FP8X4),
-                scales=scales[:],
-                in_=grouped[:].rearrange("p c i -> p (c i)"),
-            )
-            return codes, scales
+                nc.vector.tensor_copy(out=target, in_=source)
+            else:
+                nc.scalar.activation(out=target, in_=source, func=COPY)
 
-        def look_up(g):
-            both = keep.tile([P, J], U32, name=f"both{g}", align_bytes=64)
+        def new_codes(name, tag, parts=1, width=HALF):
+            return keep.tile([P, parts, width], U32, name=name, tag=tag, align_bytes=64)
+
+        def quantize(grouped, name, codes):
+            width = grouped.shape[1]
+            scales = keep.tile([P, width], U8, name=name + "_scales", align_bytes=64)
+            nc.vector.quantize_mx(
+                out=codes.bitcast(FP8X4),
+                scales=scales[:],
+                in_=grouped.rearrange("p c i -> p (c i)"),
+            )
+            return codes, scales[:]
+
+        def look_up(g, tag):
+            both = keep.tile([P, J], U32, name=f"both{g}", tag=tag, align_bytes=64)
             entries = offsets[:, g * LIST_COLUMNS : (g + 1) * LIST_COLUMNS]
             nc.vector.tensor_copy(both[:], word_window[:].bitcast(U32).indirect(entries))
-            apart = keep.tile([P, PASSES, 2 * J], U8, name=f"apart{g}", align_bytes=64)
+            return both
+
+        def part(both, g, tag):
+            apart = keep.tile([P, PASSES, 2 * J], U8, name=f"apart{g}", tag=tag, align_bytes=64)
             nc.vector.tensor_copy(
                 out=apart[:].bitcast(U16),
                 in_=both[:].bitcast(U16).rearrange("p (j a) -> p a j", a=PASSES),
             )
             return apart
 
-        wq = [quantize(w_raw[0], "w0", "reused")]
-        picked = [look_up(g) for g in range(G)]
-        wq.append(quantize(w_raw[1], "w1", "w1_codes"))
-        iw_cols = keep.tile([P, P], F32, name="iw_cols", align_bytes=64)
-        nc.vector.transpose(iw_cols[:], iw_rows[:])
-        xq = [
-            quantize(x_raw[0], "x0", "x0_codes", X0_ON_VECTOR),
-            quantize(x_raw[1], "x1", "x1_codes"),
-        ]
+        def bank(b, name):
+            return psum.tile([P, N], F32, name=name, tag=f"bank{b}")
+
+        halves = [slice(0, HALF), slice(HALF, WIDTH)]
+
+        iw_turned = bank(PSUM_BANKS - 1, "iw_turned")
+        nc.tensor.transpose(iw_turned[:, 0:P], iw_rows[:], ident[:])
+        iw_cols = keep.tile([P, G * TILES], F32, name="iw_cols")
+        nc.scalar.copy(out=iw_cols[:], in_=iw_turned[:, 0 : G * TILES])
+
+        w_bf16 = []
+        for a in range(PASSES):
+            name = f"w{a}_bf16"
+            w_bf16.append(keep.tile([P, WIDTH, PACK], BF16, name=name, tag=name, align_bytes=64))
+            cast(w_bf16[a][:], w_raw[a][:])
+        wq = [quantize(w_bf16[0][:], "w0", new_codes("w0_codes", "reused", 1, WIDTH)[:, 0, :])]
+        gathered = [look_up(g, f"both{g}") for g in range(G - 1)]
+        picked = [part(gathered[g], g, f"apart{g}") for g in range(G - 1)]
+        gathered.append(look_up(G - 1, f"both{G - 2}"))
+        w1_codes = new_codes("w1_codes", "w1_codes", 1, WIDTH)
+        wq.append(quantize(w_bf16[1][:], "w1", w1_codes[:, 0, :]))
+        picked.append(part(gathered[G - 1], G - 1, "w1_bf16"))
+
+        idle = bank(PSUM_BANKS - 1, "idle")
+        for rep in range(WARM_UP_PASSES):
+            nc.tensor.matmul_mx(
+                out=idle[:],
+                lhsT=gathered[0][:].bitcast(U8)[:, 0 : 2 * P].bitcast(FP4X4),
+                lhsT_scale=wq[0][1][:, 0:P],
+                rhs=wq[0][0].bitcast(FP8X4),
+                rhs_scale=wq[0][1],
+                start=True,
+                stop=True,
+            )
 
         tab_scale_bytes = tab_scale[:].bitcast(U8)
+
+        def look_up_pass(acc, g, jt, a):
+            nc.tensor.matmul_mx(
+                out=acc[:],
+                lhsT=picked[g][:, a, 2 * P * jt : 2 * P * (jt + 1)].bitcast(FP4X4),
+                lhsT_scale=tab_scale_bytes[:, a, g * J + P * jt : g * J + P * (jt + 1)],
+                rhs=wq[a][0].bitcast(FP8X4),
+                rhs_scale=wq[a][1],
+                start=(a == 0),
+                stop=(a == PASSES - 1),
+            )
+
         partial = [None] * TILES
 
-        def add_look_up(g, jt):
-            acc = psum.tile([P, N], F32, name="bank")
-            for a in range(PASSES):
-                nc.tensor.matmul_mx(
-                    out=acc[:],
-                    lhsT=picked[g][:, a, 2 * P * jt : 2 * P * (jt + 1)].bitcast(FP4X4),
-                    lhsT_scale=tab_scale_bytes[:, a, g * J + P * jt : g * J + P * (jt + 1)],
-                    rhs=wq[a][0][:].bitcast(FP8X4),
-                    rhs_scale=wq[a][1][:],
-                    start=(a == 0),
-                    stop=(a == PASSES - 1),
-                )
-            weight = iw_cols[:, QUAD * jt + g : QUAD * jt + g + 1]
-            total = keep.tile([P, N], F32, name=f"partial{g}_{jt}")
+        def weigh(acc, g, jt):
+            weight = iw_cols[:, TILES * g + jt : TILES * g + jt + 1]
+            name = f"partial{g}_{jt}"
+            place = TILES * (g - 1) + jt - 2
+            tag = f"partial{place // TILES}_{place % TILES}" if g == G - 1 else name
+            total = keep.tile([P, N], F32, name=name, tag=tag, align_bytes=64)
             if g == 0:
                 nc.scalar.activation(out=total[:], in_=acc[:], func=COPY, scale=weight)
             else:
@@ -189,51 +221,78 @@ def tile_list_interp_none_kernel(
                 )
             partial[jt] = total
 
-        steps = [(g, half) for g in range(G) for half in range(2)]
-        for g, half in sorted(steps, key=lambda s: 2 * s[0] + 3 * s[1]):
-            for jt in (2 * half, 2 * half + 1):
-                add_look_up(g, jt)
+        x00_bf16 = keep.tile([P, HALF, PACK], BF16, name="x00_bf16", align_bytes=64)
+        cast(x00_bf16[:], x_raw[0][:, :, halves[0]], on_vector=True)
 
-        wx_scale_bytes = wx_scale[:].bitcast(U8)
-
-        def dense_pass(acc, nt, a):
-            nc.tensor.matmul_mx(
-                out=acc[:],
-                lhsT=wx_word[:, a, P * nt : P * (nt + 1)].bitcast(FP8X4),
-                lhsT_scale=wx_scale_bytes[:, a, P * nt : P * (nt + 1)],
-                rhs=xq[a][0][:].bitcast(FP8X4),
-                rhs_scale=xq[a][1][:],
-                start=(a == 0),
-                stop=(a == PASSES - 1),
-            )
-
-        dense = []
-        for nt in range(DENSE_AHEAD):
-            acc = psum.tile([P, J], F32, name="bank")
-            dense_pass(acc, nt, 0)
-            dense.append(acc)
-
-        turned = [psum.tile([P, J], F32, name="bank") for nt in range(TILES)]
+        early = {}
+        for g in range(G - 1):
+            for jt in range(TILES):
+                early[g, jt] = bank(TILES * g + jt, f"sum{g}_{jt}")
+                look_up_pass(early[g, jt], g, jt, 0)
         for jt in range(TILES):
+            for g in range(G - 1):
+                look_up_pass(early[g, jt], g, jt, 1)
+                weigh(early[g, jt], g, jt)
+
+        x01_bf16 = keep.tile(
+            [P, HALF, PACK], BF16, name="x01_bf16", tag="partial0_0", align_bytes=64
+        )
+        cast(x01_bf16[:], x_raw[0][:, :, halves[1]])
+        x1_bf16 = keep.tile(
+            [P, WIDTH, PACK], BF16, name="x1_bf16", tag="partial0_1", align_bytes=64
+        )
+        for h in range(HALVES):
+            cast(x1_bf16[:, halves[h], :], x_raw[1][:, :, halves[h]])
+        for jt in range(TILES):
+            acc = bank(jt % (TILES - 1), f"sum2_{jt}")
+            for a in range(PASSES):
+                look_up_pass(acc, G - 1, jt, a)
+            weigh(acc, G - 1, jt)
+
+        first_codes = new_codes("first_codes", "partial1_2", PASSES)
+        xq = {(0, 0): quantize(x00_bf16[:], "x00", first_codes[:, 0, :])}
+        xq[1, 0] = quantize(x1_bf16[:, halves[0], :], "x10", first_codes[:, 1, :])
+        last_codes = new_codes("last_codes", "partial1_3", PASSES)
+        xq[0, 1] = quantize(x01_bf16[:], "x01", last_codes[:, 0, :])
+        xq[1, 1] = quantize(x1_bf16[:, halves[1], :], "x11", last_codes[:, 1, :])
+
+        pieces = [(h, u) for h in range(HALVES) for u in range(HALVES)]
+
+        def by_tile(t):
+            return t[:].rearrange("p (t j) -> p t j", t=HALVES)
+
+        turned = {piece: bank(TILES + b, f"turned{b}") for b, piece in enumerate(pieces)}
+        for jt in range(TILES):
+            h, first = jt // HALVES, P * (jt % HALVES)
             for nt in range(TILES):
                 nc.tensor.transpose(
-                    turned[nt][:, P * jt : P * (jt + 1)],
+                    by_tile(turned[h, nt // HALVES])[:, nt % HALVES, first : first + P],
                     partial[jt][:, P * nt : P * (nt + 1)],
                     ident[:],
                 )
-        interpolated = keep.tile([P, TILES, J], F32, name="interpolated")
-        for nt in range(TILES):
-            nc.scalar.copy(out=interpolated[:, nt, :], in_=turned[nt][:])
+        interpolated = {}
+        for b, piece in enumerate(pieces):
+            interpolated[piece] = keep.tile([P, N], F32, name=f"interpolated{b}")
+            nc.scalar.copy(out=interpolated[piece][:], in_=turned[piece][:])
 
-        for nt in range(TILES):
-            if nt >= DENSE_AHEAD:
-                acc = psum.tile([P, J], F32, name="bank")
-                dense_pass(acc, nt, 0)
-                dense.append(acc)
-            dense_pass(dense[nt], nt, 1)
-        for nt in range(TILES):
-            result = keep.tile([P, J], F32, name=f"result{nt}")
+        wx_scale_bytes = wx_scale[:].bitcast(U8)
+        for b, (h, u) in enumerate(pieces):
+            dense = bank((b - 1) % TILES if b < 1 else b % (TILES - 1), f"dense{b}")
+            for t in range(HALVES):
+                nt = HALVES * u + t
+                for a in range(PASSES):
+                    nc.tensor.matmul_mx(
+                        out=by_tile(dense)[:, t, :],
+                        lhsT=wx_word[:, a, P * nt : P * (nt + 1)].bitcast(FP8X4),
+                        lhsT_scale=wx_scale_bytes[:, a, P * nt : P * (nt + 1)],
+                        rhs=xq[a, h][0].bitcast(FP8X4),
+                        rhs_scale=xq[a, h][1],
+                        start=(a == 0),
+                        stop=(a == PASSES - 1),
+                    )
+            result = keep.tile([P, J], F32, name=f"result{b}")
             nc.vector.tensor_tensor(
-                out=result[:], in0=dense[nt][:], in1=interpolated[:, nt, :], op=ADD
+                out=result[:], in0=dense[:], in1=interpolated[h, u][:], op=ADD
             )
-            nc.sync.dma_start(out=out[P * nt : P * (nt + 1), :], in_=result[:])
+            rows = out[HALVES * P * u : HALVES * P * (u + 1), halves[h]]
+            nc.sync.dma_start(out=rows.rearrange("(t p) j -> p t j", p=P), in_=by_tile(result))

@@ -43,6 +43,7 @@ def tile_list_interp_none_kernel(
     with ExitStack() as ctx:
         lists = ctx.enter_context(tc.tile_pool(name="lists", bufs=1))
         keep = ctx.enter_context(tc.tile_pool(name="keep", bufs=1))
+        shared = ctx.enter_context(tc.tile_pool(name="shared", bufs=1))
         psum = ctx.enter_context(tc.psum_pool(name="psum", bufs=1))
 
         scale_window = keep.tile(
@@ -58,13 +59,20 @@ def tile_list_interp_none_kernel(
         tab_scale = keep.tile([P, PASSES, G * J // 4], I32, name="tab_scale", align_bytes=64)
         nc.vector.memset(tab_scale[:], 0)
 
-        def load_pass(src, a, name):
-            raw = keep.tile([P, PACK, WIDTH], F32, name=name)
-            rows = src[a * K_PASS : (a + 1) * K_PASS, :]
+        whole = slice(0, WIDTH)
+        halves = [slice(0, HALF), slice(HALF, WIDTH)]
+
+        def load_pass(src, a, cols, name, reused=False):
+            shape = [P, PACK, cols.stop - cols.start]
+            if reused:
+                raw = shared.tile(shape, F32, name=name, offset=0)
+            else:
+                raw = keep.tile(shape, F32, name=name)
+            rows = src[a * K_PASS : (a + 1) * K_PASS, cols]
             nc.sync.dma_start(out=raw[:], in_=rows.rearrange("(p i) c -> p i c", i=PACK))
             return raw
 
-        w_raw = [load_pass(w, 0, "w_raw0")]
+        w0_raw = load_pass(w, 0, whole, "w0_raw")
 
         offsets = lists.tile([P, G * LIST_COLUMNS], U16, name="offsets")
         nc.sync.dma_start(offsets[:], offs)
@@ -73,16 +81,16 @@ def tile_list_interp_none_kernel(
             out=scale_window[0:P:SPREAD, :],
             in_=tab_scales.bitcast(I32).rearrange("a s t -> (a s) t"),
         )
-        word_window = keep.tile([P, T], I32, name="word_window", align_bytes=64)
-        nc.sync.dma_start(
-            out=word_window[:], in_=tab_words[0].rearrange("p t b -> p (t b)").bitcast(I32)
-        )
         for g, vec in enumerate((iw0, iw1, iw2)):
             nc.sync.dma_start(
                 out=iw_rows[TILES * g : TILES * (g + 1), :],
                 in_=vec.rearrange("(c p) -> c p", p=P),
             )
-        w_raw.append(load_pass(w, 1, "w_raw1"))
+        word_window = keep.tile([P, T], I32, name="word_window", align_bytes=64)
+        nc.sync.dma_start(
+            out=word_window[:], in_=tab_words[0].rearrange("p t b -> p (t b)").bitcast(I32)
+        )
+        w1_raw = [load_pass(w, 1, halves[0], "w10_raw")]
 
         picked_scales = keep.tile([P, G * J], U8, name="picked_scales", align_bytes=64)
         nc.vector.tensor_copy(picked_scales[:], scale_window[:].bitcast(U8).indirect(offsets[:]))
@@ -97,9 +105,13 @@ def tile_list_interp_none_kernel(
                 )
 
         place_scales(0)
-        x_raw = [load_pass(x, 0, "x_raw0")]
+        w1_raw.append(load_pass(w, 1, halves[1], "w11_raw"))
         place_scales(1)
-        x_raw.append(load_pass(x, 1, "x_raw1"))
+        x0_raw = [
+            load_pass(x, 0, halves[0], "x00_raw", reused=True),
+            load_pass(x, 0, halves[1], "x01_raw"),
+        ]
+        x1_raw = load_pass(x, 1, whole, "x1_raw")
         wx_word = keep.tile([P, PASSES, N], I32, name="wx_word", align_bytes=64)
         nc.sync.dma_start(
             out=wx_word[:], in_=wx_words.rearrange("a p n b -> p a (n b)").bitcast(I32)
@@ -160,8 +172,6 @@ def tile_list_interp_none_kernel(
         def bank(b, name):
             return psum.tile([P, N], F32, name=name, tag=f"bank{b}")
 
-        halves = [slice(0, HALF), slice(HALF, WIDTH)]
-
         iw_turned = bank(PSUM_BANKS - 1, "iw_turned")
         nc.tensor.transpose(iw_turned[:, 0:P], iw_rows[:], ident[:])
         iw_cols = keep.tile([P, G * TILES], F32, name="iw_cols")
@@ -171,7 +181,9 @@ def tile_list_interp_none_kernel(
         for a in range(PASSES):
             name = f"w{a}_bf16"
             w_bf16.append(keep.tile([P, WIDTH, PACK], BF16, name=name, tag=name, align_bytes=64))
-            cast(w_bf16[a][:], w_raw[a][:])
+        cast(w_bf16[0][:], w0_raw[:])
+        for h in range(HALVES):
+            cast(w_bf16[1][:, halves[h], :], w1_raw[h][:])
         wq = [quantize(w_bf16[0][:], "w0", new_codes("w0_codes", "reused", 1, WIDTH)[:, 0, :])]
         gathered = [look_up(g, f"both{g}") for g in range(G - 1)]
         picked = [part(gathered[g], g, f"apart{g}") for g in range(G - 1)]
@@ -212,7 +224,10 @@ def tile_list_interp_none_kernel(
             name = f"partial{g}_{jt}"
             place = TILES * (g - 1) + jt - 2
             tag = f"partial{place // TILES}_{place % TILES}" if g == G - 1 else name
-            total = keep.tile([P, N], F32, name=name, tag=tag, align_bytes=64)
+            if g > 0 and jt // 2 == g - 1:
+                total = shared.tile([P, N], F32, name=name, offset=4 * N * (jt % 2))
+            else:
+                total = keep.tile([P, N], F32, name=name, tag=tag, align_bytes=64)
             if g == 0:
                 nc.scalar.activation(out=total[:], in_=acc[:], func=COPY, scale=weight)
             else:
@@ -222,7 +237,7 @@ def tile_list_interp_none_kernel(
             partial[jt] = total
 
         x00_bf16 = keep.tile([P, HALF, PACK], BF16, name="x00_bf16", align_bytes=64)
-        cast(x00_bf16[:], x_raw[0][:, :, halves[0]], on_vector=True)
+        cast(x00_bf16[:], x0_raw[0][:], on_vector=True)
 
         early = {}
         for g in range(G - 1):
@@ -237,12 +252,12 @@ def tile_list_interp_none_kernel(
         x01_bf16 = keep.tile(
             [P, HALF, PACK], BF16, name="x01_bf16", tag="partial0_0", align_bytes=64
         )
-        cast(x01_bf16[:], x_raw[0][:, :, halves[1]])
+        cast(x01_bf16[:], x0_raw[1][:])
         x1_bf16 = keep.tile(
             [P, WIDTH, PACK], BF16, name="x1_bf16", tag="partial0_1", align_bytes=64
         )
         for h in range(HALVES):
-            cast(x1_bf16[:, halves[h], :], x_raw[1][:, :, halves[h]])
+            cast(x1_bf16[:, halves[h], :], x1_raw[:, :, halves[h]])
         for jt in range(TILES):
             acc = bank(jt % (TILES - 1), f"sum2_{jt}")
             for a in range(PASSES):

@@ -1,6 +1,7 @@
 from contextlib import ExitStack
 
 import concourse.mybir as mybir
+from concourse.masks import make_identity
 
 K, L, N, T, J = 1024, 1024, 512, 4096, 512
 G = 3
@@ -17,7 +18,6 @@ FP4X4 = mybir.dt.float4_e2m1fn_x4
 COPY = mybir.ActivationFunctionType.Copy
 MULT = mybir.AluOpType.mult
 ADD = mybir.AluOpType.add
-EQUAL = mybir.AluOpType.is_equal
 
 P = 128
 QUAD = 32
@@ -28,10 +28,13 @@ PASSES = 2
 WIDTH = 512
 TILES = 4
 ROWS_A_QUAD = 4
-SPREAD = 4
+FIRST_ROW = 96
 LIST_COLUMNS = J // 16
 PSUM_BANKS = 8
-WARM_UP_PASSES = 3
+WARM_UP_WIDTHS = (512, 512, 256, 256)
+OPENED_EARLY = 7
+W1_ON_VECTOR = 128
+SPLIT_TILES = (3,)
 HALVES = 2
 HALF = WIDTH // HALVES
 
@@ -43,96 +46,78 @@ def tile_list_interp_none_kernel(
     with ExitStack() as ctx:
         lists = ctx.enter_context(tc.tile_pool(name="lists", bufs=1))
         keep = ctx.enter_context(tc.tile_pool(name="keep", bufs=1))
-        shared = ctx.enter_context(tc.tile_pool(name="shared", bufs=1))
         psum = ctx.enter_context(tc.psum_pool(name="psum", bufs=1))
 
-        scale_window = keep.tile(
-            [P, T // 4], I32, name="scale_window", tag="reused", align_bytes=64
-        )
-        nc.vector.memset(scale_window[:], 0)
-        ident = keep.tile([P, P], F32, name="ident")
-        nc.vector.memset(ident[:], 0.0)
-        iw_rows = keep.tile([P, P], F32, name="iw_rows", align_bytes=64)
-        nc.scalar.activation(out=iw_rows[:], in_=ident[:], func=COPY)
-        wx_scale = keep.tile([P, PASSES, N // 4], I32, name="wx_scale", align_bytes=64)
-        nc.vector.memset(wx_scale[:], 0)
-        tab_scale = keep.tile([P, PASSES, G * J // 4], I32, name="tab_scale", align_bytes=64)
-        nc.vector.memset(tab_scale[:], 0)
+        def sbuf(shape, dtype, name, tag=None):
+            return keep.tile(shape, dtype, name=name, tag=tag or name, align_bytes=64)
 
-        whole = slice(0, WIDTH)
+        scale_window = sbuf([P, T // 4], I32, "scale_window")
+        nc.vector.memset(scale_window[0 : 2 * QUAD, :], 0)
+        nc.vector.memset(scale_window[2 * QUAD : FIRST_ROW, :], 0)
+        iw_rows = sbuf([P, P], F32, "iw_rows")
+        nc.gpsimd.memset(iw_rows[:], 0.0)
+        tab_scale = [sbuf([P, G * J // 4], I32, f"tab_scale{a}") for a in range(PASSES)]
+        for a in range(PASSES):
+            nc.vector.memset(tab_scale[a][:], 0)
+        wx_scale = sbuf([P, PASSES, N // 4], I32, "wx_scale")
+        nc.vector.memset(wx_scale[:], 0)
+        ident = sbuf([P, P], F32, "ident")
+        make_identity(nc, ident[:])
+
         halves = [slice(0, HALF), slice(HALF, WIDTH)]
 
-        def load_pass(src, a, cols, name, reused=False):
-            shape = [P, PACK, cols.stop - cols.start]
-            if reused:
-                raw = shared.tile(shape, F32, name=name, offset=0)
-            else:
-                raw = keep.tile(shape, F32, name=name)
+        whole = slice(0, WIDTH)
+
+        def load(src, a, cols, name):
+            raw = sbuf([P, PACK, cols.stop - cols.start], F32, name)
             rows = src[a * K_PASS : (a + 1) * K_PASS, cols]
             nc.sync.dma_start(out=raw[:], in_=rows.rearrange("(p i) c -> p i c", i=PACK))
             return raw
 
-        w0_raw = load_pass(w, 0, whole, "w0_raw")
-
         offsets = lists.tile([P, G * LIST_COLUMNS], U16, name="offsets")
         nc.sync.dma_start(offsets[:], offs)
-
         nc.sync.dma_start(
-            out=scale_window[0:P:SPREAD, :],
+            out=scale_window[FIRST_ROW:P, :],
             in_=tab_scales.bitcast(I32).rearrange("a s t -> (a s) t"),
         )
+        w0_raw = load(w, 0, whole, "w0_raw")
         for g, vec in enumerate((iw0, iw1, iw2)):
             nc.sync.dma_start(
                 out=iw_rows[TILES * g : TILES * (g + 1), :],
                 in_=vec.rearrange("(c p) -> c p", p=P),
             )
-        word_window = keep.tile([P, T], I32, name="word_window", align_bytes=64)
+        word_window = sbuf([P, T], I32, "word_window")
         nc.sync.dma_start(
             out=word_window[:], in_=tab_words[0].rearrange("p t b -> p (t b)").bitcast(I32)
         )
-        w1_raw = [load_pass(w, 1, halves[0], "w10_raw")]
 
-        picked_scales = keep.tile([P, G * J], U8, name="picked_scales", align_bytes=64)
+        picked_scales = sbuf([P, G * J], U8, "picked_scales")
         nc.vector.tensor_copy(picked_scales[:], scale_window[:].bitcast(U8).indirect(offsets[:]))
 
         def place_scales(a):
-            first = a * QUADS * ROWS_A_QUAD * SPREAD
-            step = ROWS_A_QUAD * SPREAD
+            first = FIRST_ROW + a * QUADS * ROWS_A_QUAD
             for r in range(ROWS_A_QUAD):
-                rows = slice(first + SPREAD * r, first + QUADS * step, step)
+                rows = slice(first + r, first + QUADS * ROWS_A_QUAD, ROWS_A_QUAD)
                 nc.sync.dma_start(
-                    out=tab_scale[r:P:QUAD, a, :], in_=picked_scales[rows, :].bitcast(I32)
+                    out=tab_scale[a][r:P:QUAD, :], in_=picked_scales[rows, :].bitcast(I32)
                 )
 
         place_scales(0)
-        w1_raw.append(load_pass(w, 1, halves[1], "w11_raw"))
+        w1_raw = keep.tile([P, PACK, WIDTH], F32, name="w1_raw", tag="scale_window", align_bytes=64)
+        nc.sync.dma_start(
+            out=w1_raw[:], in_=w[K_PASS : 2 * K_PASS, :].rearrange("(p i) c -> p i c", i=PACK)
+        )
         place_scales(1)
-        x0_raw = [
-            load_pass(x, 0, halves[0], "x00_raw", reused=True),
-            load_pass(x, 0, halves[1], "x01_raw"),
-        ]
-        x1_raw = load_pass(x, 1, whole, "x1_raw")
-        wx_word = keep.tile([P, PASSES, N], I32, name="wx_word", align_bytes=64)
+        x_raw = {}
+        for a, h in ((0, 0), (1, 0), (0, 1), (1, 1)):
+            x_raw[a, h] = load(x, a, halves[h], f"x{a}{h}_raw")
+        wx_word = sbuf([P, PASSES, N], I32, "wx_word")
         nc.sync.dma_start(
             out=wx_word[:], in_=wx_words.rearrange("a p n b -> p a (n b)").bitcast(I32)
         )
         wx_scale_rows = wx_scales.bitcast(I32).rearrange("a (q r) n -> r q a n", r=ROWS_A_QUAD)
         for r in range(ROWS_A_QUAD):
             nc.sync.dma_start(out=wx_scale[r:P:QUAD, :, :], in_=wx_scale_rows[r])
-
-        ones = keep.tile([P, P], F32, name="ones")
-        nc.vector.memset(ones[:], 1.0)
-        ramp = keep.tile([P, P], F32, name="ramp", align_bytes=64)
-        nc.vector.tensor_tensor_scan(
-            out=ramp[:], data0=ones[:], data1=ones[:], initial=0.0, op0=MULT, op1=ADD
-        )
-        ramp_turned = keep.tile([P, P], F32, name="ramp_turned", align_bytes=64)
-        nc.vector.transpose(ramp_turned[:], ramp[:])
-        for q in range(QUADS):
-            blk = slice(QUAD * q, QUAD * (q + 1))
-            nc.vector.tensor_tensor(
-                out=ident[blk, blk], in0=ramp[blk, blk], in1=ramp_turned[blk, blk], op=EQUAL
-            )
 
         def cast(grouped, raw, on_vector=False):
             target = grouped.rearrange("p (c u) i -> p c i u", u=4)
@@ -142,27 +127,21 @@ def tile_list_interp_none_kernel(
             else:
                 nc.scalar.activation(out=target, in_=source, func=COPY)
 
-        def new_codes(name, tag, parts=1, width=HALF):
-            return keep.tile([P, parts, width], U32, name=name, tag=tag, align_bytes=64)
-
-        def quantize(grouped, name, codes):
-            width = grouped.shape[1]
-            scales = keep.tile([P, width], U8, name=name + "_scales", align_bytes=64)
+        def quantize(grouped, codes, scales):
             nc.vector.quantize_mx(
                 out=codes.bitcast(FP8X4),
-                scales=scales[:],
+                scales=scales,
                 in_=grouped.rearrange("p c i -> p (c i)"),
             )
-            return codes, scales[:]
 
         def look_up(g, tag):
-            both = keep.tile([P, J], U32, name=f"both{g}", tag=tag, align_bytes=64)
+            both = sbuf([P, J], U32, f"both{g}", tag)
             entries = offsets[:, g * LIST_COLUMNS : (g + 1) * LIST_COLUMNS]
             nc.vector.tensor_copy(both[:], word_window[:].bitcast(U32).indirect(entries))
             return both
 
-        def part(both, g, tag):
-            apart = keep.tile([P, PASSES, 2 * J], U8, name=f"apart{g}", tag=tag, align_bytes=64)
+        def part(both, g):
+            apart = sbuf([P, PASSES, 2 * J], U8, f"apart{g}")
             nc.vector.tensor_copy(
                 out=apart[:].bitcast(U16),
                 in_=both[:].bitcast(U16).rearrange("p (j a) -> p a j", a=PASSES),
@@ -172,104 +151,121 @@ def tile_list_interp_none_kernel(
         def bank(b, name):
             return psum.tile([P, N], F32, name=name, tag=f"bank{b}")
 
+        w_codes = [sbuf([P, WIDTH], U32, f"w{a}_codes") for a in range(PASSES)]
+        w_scales = [sbuf([P, WIDTH], U8, f"w{a}_scales") for a in range(PASSES)]
+
+        def prepare_w(raw, a, cols, name):
+            grouped = sbuf([P, raw.shape[2], PACK], BF16, name)
+            cast(grouped[:], raw)
+            quantize(grouped[:], w_codes[a][:, cols], w_scales[a][:, cols])
+
+        prepare_w(w0_raw[:], 0, whole, "w0_bf16")
         iw_turned = bank(PSUM_BANKS - 1, "iw_turned")
         nc.tensor.transpose(iw_turned[:, 0:P], iw_rows[:], ident[:])
-        iw_cols = keep.tile([P, G * TILES], F32, name="iw_cols")
+        iw_cols = sbuf([P, G * TILES], F32, "iw_cols")
         nc.scalar.copy(out=iw_cols[:], in_=iw_turned[:, 0 : G * TILES])
 
-        w_bf16 = []
-        for a in range(PASSES):
-            name = f"w{a}_bf16"
-            w_bf16.append(keep.tile([P, WIDTH, PACK], BF16, name=name, tag=name, align_bytes=64))
-        cast(w_bf16[0][:], w0_raw[:])
-        for h in range(HALVES):
-            cast(w_bf16[1][:, halves[h], :], w1_raw[h][:])
-        wq = [quantize(w_bf16[0][:], "w0", new_codes("w0_codes", "reused", 1, WIDTH)[:, 0, :])]
-        gathered = [look_up(g, f"both{g}") for g in range(G - 1)]
-        picked = [part(gathered[g], g, f"apart{g}") for g in range(G - 1)]
-        gathered.append(look_up(G - 1, f"both{G - 2}"))
-        w1_codes = new_codes("w1_codes", "w1_codes", 1, WIDTH)
-        wq.append(quantize(w_bf16[1][:], "w1", w1_codes[:, 0, :]))
-        picked.append(part(gathered[G - 1], G - 1, "w1_bf16"))
+        gathered = [look_up(0, None)]
+        picked = [part(gathered[0], 0)]
+        gathered.append(look_up(1, None))
+        picked.append(part(gathered[1], 1))
+        w1_last = sbuf([P, HALF, PACK], BF16, "w11_bf16")
+        own = HALF - W1_ON_VECTOR
+        cast(w1_last[:, own:HALF, :], w1_raw[:, :, HALF + own : WIDTH], on_vector=True)
+        prepare_w(w1_raw[:, :, halves[0]], 1, halves[0], "w10_bf16")
+        cast(w1_last[:, 0:own, :], w1_raw[:, :, HALF : HALF + own])
+        quantize(w1_last[:], w_codes[1][:, halves[1]], w_scales[1][:, halves[1]])
+        gathered.append(look_up(2, "scale_window"))
+        picked.append(part(gathered[2], 2))
 
-        idle = bank(PSUM_BANKS - 1, "idle")
-        for rep in range(WARM_UP_PASSES):
+        tab_scale_bytes = [t[:].bitcast(U8) for t in tab_scale]
+        for b, width in enumerate(WARM_UP_WIDTHS):
+            idle = bank(b, f"idle{b}")
             nc.tensor.matmul_mx(
-                out=idle[:],
-                lhsT=gathered[0][:].bitcast(U8)[:, 0 : 2 * P].bitcast(FP4X4),
-                lhsT_scale=wq[0][1][:, 0:P],
-                rhs=wq[0][0].bitcast(FP8X4),
-                rhs_scale=wq[0][1],
+                out=idle[:, 0:width],
+                lhsT=w_codes[0][:, 0:P].bitcast(FP8X4),
+                lhsT_scale=w_scales[0][:, 0:P],
+                rhs=word_window[:].bitcast(U8)[:, 0 : 2 * width].bitcast(FP4X4),
+                rhs_scale=tab_scale_bytes[0][:, 0:width],
                 start=True,
                 stop=True,
             )
 
-        tab_scale_bytes = tab_scale[:].bitcast(U8)
-
-        def look_up_pass(acc, g, jt, a):
+        def look_up_pass(acc, g, jt, a, first=0):
             nc.tensor.matmul_mx(
                 out=acc[:],
                 lhsT=picked[g][:, a, 2 * P * jt : 2 * P * (jt + 1)].bitcast(FP4X4),
-                lhsT_scale=tab_scale_bytes[:, a, g * J + P * jt : g * J + P * (jt + 1)],
-                rhs=wq[a][0].bitcast(FP8X4),
-                rhs_scale=wq[a][1],
-                start=(a == 0),
-                stop=(a == PASSES - 1),
+                lhsT_scale=tab_scale_bytes[a][:, g * J + P * jt : g * J + P * (jt + 1)],
+                rhs=w_codes[a][:].bitcast(FP8X4),
+                rhs_scale=w_scales[a][:],
+                start=(a == first),
+                stop=(a != first),
             )
 
         partial = [None] * TILES
+        spare = {}
 
-        def weigh(acc, g, jt):
+        def weigh(acc, g, jt, tag=None):
             weight = iw_cols[:, TILES * g + jt : TILES * g + jt + 1]
-            name = f"partial{g}_{jt}"
-            place = TILES * (g - 1) + jt - 2
-            tag = f"partial{place // TILES}_{place % TILES}" if g == G - 1 else name
-            if g > 0 and jt // 2 == g - 1:
-                total = shared.tile([P, N], F32, name=name, offset=4 * N * (jt % 2))
+            if g == 0 or (g == 1 and jt in SPLIT_TILES):
+                total = terms[:, jt if g == 0 else TILES + SPLIT_TILES.index(jt), :]
+                nc.scalar.activation(out=total, in_=acc[:], func=COPY, scale=weight)
+                if g == 1:
+                    spare[jt] = partial[jt]
             else:
-                total = keep.tile([P, N], F32, name=name, tag=tag, align_bytes=64)
-            if g == 0:
-                nc.scalar.activation(out=total[:], in_=acc[:], func=COPY, scale=weight)
-            else:
+                total = sbuf([P, N], F32, f"partial{g}_{jt}", tag)[:]
                 nc.vector.scalar_tensor_tensor(
-                    out=total[:], in0=acc[:], scalar=weight, in1=partial[jt][:], op0=MULT, op1=ADD
+                    out=total, in0=acc[:], scalar=weight, in1=partial[jt], op0=MULT, op1=ADD
                 )
             partial[jt] = total
 
-        x00_bf16 = keep.tile([P, HALF, PACK], BF16, name="x00_bf16", align_bytes=64)
-        cast(x00_bf16[:], x0_raw[0][:], on_vector=True)
-
+        x_first = sbuf([P, HALF, PACK], BF16, "x_first")
+        cast(x_first[:], x_raw[0, 0][:])
+        terms = sbuf([P, TILES + len(SPLIT_TILES), N], F32, "terms", "x00_raw")
         early = {}
         for g in range(G - 1):
             for jt in range(TILES):
                 early[g, jt] = bank(TILES * g + jt, f"sum{g}_{jt}")
-                look_up_pass(early[g, jt], g, jt, 0)
+                if TILES * g + jt < OPENED_EARLY:
+                    look_up_pass(early[g, jt], g, jt, 0)
         for jt in range(TILES):
             for g in range(G - 1):
-                look_up_pass(early[g, jt], g, jt, 1)
-                weigh(early[g, jt], g, jt)
+                if TILES * g + jt < OPENED_EARLY:
+                    look_up_pass(early[g, jt], g, jt, 1)
+                    weigh(early[g, jt], g, jt)
+        for late in reversed(range(OPENED_EARLY, PSUM_BANKS)):
+            g, jt = divmod(late, TILES)
+            for a in (1, 0):
+                look_up_pass(early[g, jt], g, jt, a, first=1)
+            weigh(early[g, jt], g, jt)
 
-        x01_bf16 = keep.tile(
-            [P, HALF, PACK], BF16, name="x01_bf16", tag="partial0_0", align_bytes=64
-        )
-        cast(x01_bf16[:], x0_raw[1][:])
-        x1_bf16 = keep.tile(
-            [P, WIDTH, PACK], BF16, name="x1_bf16", tag="partial0_1", align_bytes=64
-        )
-        for h in range(HALVES):
-            cast(x1_bf16[:, halves[h], :], x1_raw[:, :, halves[h]])
-        for jt in range(TILES):
+        codes = [sbuf([P, PASSES * HALF], U32, f"x_codes{h}") for h in range(HALVES)]
+        scales = [sbuf([P, PASSES * HALF], U8, f"x{h}_scales") for h in range(HALVES)]
+        quantize(x_first[:], codes[0][:, halves[0]], scales[0][:, halves[0]])
+        x_second = sbuf([P, HALF, PACK], BF16, "x_second", "apart1")
+        cast(x_second[:], x_raw[1, 0][:])
+        x_rest = sbuf([P, PASSES * HALF, PACK], BF16, "x_rest", "x_first")
+        for a in range(PASSES):
+            nc.gpsimd.tensor_scalar(
+                x_rest[:, halves[a], :],
+                x_raw[a, 1][:].rearrange("p i c -> p c i"),
+                1.0,
+                0.0,
+                op0=MULT,
+                op1=ADD,
+            )
+        for jt, tag in enumerate((None, None, "partial1_0", "partial1_1")):
             acc = bank(jt % (TILES - 1), f"sum2_{jt}")
             for a in range(PASSES):
                 look_up_pass(acc, G - 1, jt, a)
-            weigh(acc, G - 1, jt)
+            weigh(acc, G - 1, jt, tag)
 
-        first_codes = new_codes("first_codes", "partial1_2", PASSES)
-        xq = {(0, 0): quantize(x00_bf16[:], "x00", first_codes[:, 0, :])}
-        xq[1, 0] = quantize(x1_bf16[:, halves[0], :], "x10", first_codes[:, 1, :])
-        last_codes = new_codes("last_codes", "partial1_3", PASSES)
-        xq[0, 1] = quantize(x01_bf16[:], "x01", last_codes[:, 0, :])
-        xq[1, 1] = quantize(x1_bf16[:, halves[1], :], "x11", last_codes[:, 1, :])
+        quantize(x_second[:], codes[0][:, halves[1]], scales[0][:, halves[1]])
+        quantize(x_rest[:], codes[1][:], scales[1][:])
+        xq = {}
+        for h in range(HALVES):
+            for a in range(PASSES):
+                xq[a, h] = (codes[h][:, halves[a]], scales[h][:, halves[a]])
 
         pieces = [(h, u) for h in range(HALVES) for u in range(HALVES)]
 
@@ -277,17 +273,25 @@ def tile_list_interp_none_kernel(
             return t[:].rearrange("p (t j) -> p t j", t=HALVES)
 
         turned = {piece: bank(TILES + b, f"turned{b}") for b, piece in enumerate(pieces)}
-        for jt in range(TILES):
+        sources = [(jt, spare[jt]) for jt in SPLIT_TILES] + list(enumerate(partial))
+        todo = {piece: HALVES * len([1 for jt, s in sources if jt // HALVES == piece[0]]) for piece in pieces}
+        done = {piece: 0 for piece in pieces}
+        for jt, source in sources:
             h, first = jt // HALVES, P * (jt % HALVES)
             for nt in range(TILES):
-                nc.tensor.transpose(
-                    by_tile(turned[h, nt // HALVES])[:, nt % HALVES, first : first + P],
-                    partial[jt][:, P * nt : P * (nt + 1)],
+                piece = (h, nt // HALVES)
+                nc.tensor.matmul(
+                    by_tile(turned[piece])[:, nt % HALVES, first : first + P],
+                    source[:, P * nt : P * (nt + 1)],
                     ident[:],
+                    is_transpose=True,
+                    start=(done[piece] == 0),
+                    stop=(done[piece] == todo[piece] - 1),
                 )
+                done[piece] = done[piece] + 1
         interpolated = {}
         for b, piece in enumerate(pieces):
-            interpolated[piece] = keep.tile([P, N], F32, name=f"interpolated{b}")
+            interpolated[piece] = sbuf([P, N], F32, f"interpolated{b}")
             nc.scalar.copy(out=interpolated[piece][:], in_=turned[piece][:])
 
         wx_scale_bytes = wx_scale[:].bitcast(U8)
@@ -305,7 +309,7 @@ def tile_list_interp_none_kernel(
                         start=(a == 0),
                         stop=(a == PASSES - 1),
                     )
-            result = keep.tile([P, J], F32, name=f"result{b}")
+            result = sbuf([P, J], F32, f"result{b}")
             nc.vector.tensor_tensor(
                 out=result[:], in0=dense[:], in1=interpolated[h, u][:], op=ADD
             )

@@ -26,17 +26,16 @@ PACK = 4
 K_PASS = P * PACK
 PASSES = 2
 WIDTH = 512
-TILES = 4
-ROWS_A_QUAD = 4
-FIRST_ROW = 96
-LIST_COLUMNS = J // 16
-PSUM_BANKS = 8
-WARM_UP_WIDTHS = (512, 512, 256, 256)
-OPENED_EARLY = 7
-W1_ON_VECTOR = 128
-SPLIT_TILES = (3,)
 HALVES = 2
 HALF = WIDTH // HALVES
+TILES = 4
+LAST_TILE = TILES - 1
+ROWS_A_QUAD = 4
+FIRST_ROW = P - QUAD
+LIST_COLUMNS = J // 16
+PSUM_BANKS = 8
+WARM_UP_WIDTHS = (512, 256, 256, 256)
+W1_ON_VECTOR = 128
 
 
 def tile_list_interp_none_kernel(
@@ -51,9 +50,11 @@ def tile_list_interp_none_kernel(
         def sbuf(shape, dtype, name, tag=None):
             return keep.tile(shape, dtype, name=name, tag=tag or name, align_bytes=64)
 
+        def bank(b, name):
+            return psum.tile([P, N], F32, name=name, tag=f"bank{b}")
+
         scale_window = sbuf([P, T // 4], I32, "scale_window")
-        nc.vector.memset(scale_window[0 : 2 * QUAD, :], 0)
-        nc.vector.memset(scale_window[2 * QUAD : FIRST_ROW, :], 0)
+        nc.vector.memset(scale_window[0:FIRST_ROW, :], 0)
         iw_rows = sbuf([P, P], F32, "iw_rows")
         nc.gpsimd.memset(iw_rows[:], 0.0)
         tab_scale = [sbuf([P, G * J // 4], I32, f"tab_scale{a}") for a in range(PASSES)]
@@ -64,12 +65,11 @@ def tile_list_interp_none_kernel(
         ident = sbuf([P, P], F32, "ident")
         make_identity(nc, ident[:])
 
+        whole = slice(0, WIDTH)
         halves = [slice(0, HALF), slice(HALF, WIDTH)]
 
-        whole = slice(0, WIDTH)
-
-        def load(src, a, cols, name):
-            raw = sbuf([P, PACK, cols.stop - cols.start], F32, name)
+        def load(src, a, cols, name, tag=None):
+            raw = sbuf([P, PACK, cols.stop - cols.start], F32, name, tag)
             rows = src[a * K_PASS : (a + 1) * K_PASS, cols]
             nc.sync.dma_start(out=raw[:], in_=rows.rearrange("(p i) c -> p i c", i=PACK))
             return raw
@@ -103,14 +103,12 @@ def tile_list_interp_none_kernel(
                 )
 
         place_scales(0)
-        w1_raw = keep.tile([P, PACK, WIDTH], F32, name="w1_raw", tag="scale_window", align_bytes=64)
-        nc.sync.dma_start(
-            out=w1_raw[:], in_=w[K_PASS : 2 * K_PASS, :].rearrange("(p i) c -> p i c", i=PACK)
-        )
+        w1_raw = load(w, 1, whole, "w1_raw", "scale_window")
         place_scales(1)
         x_raw = {}
-        for a, h in ((0, 0), (1, 0), (0, 1), (1, 1)):
-            x_raw[a, h] = load(x, a, halves[h], f"x{a}{h}_raw")
+        for h in range(HALVES):
+            for a in range(PASSES):
+                x_raw[a, h] = load(x, a, halves[h], f"x{a}{h}_raw")
         wx_word = sbuf([P, PASSES, N], I32, "wx_word")
         nc.sync.dma_start(
             out=wx_word[:], in_=wx_words.rearrange("a p n b -> p a (n b)").bitcast(I32)
@@ -134,49 +132,45 @@ def tile_list_interp_none_kernel(
                 in_=grouped.rearrange("p c i -> p (c i)"),
             )
 
-        def look_up(g, tag):
+        def look_up(g, tag=None):
             both = sbuf([P, J], U32, f"both{g}", tag)
             entries = offsets[:, g * LIST_COLUMNS : (g + 1) * LIST_COLUMNS]
             nc.vector.tensor_copy(both[:], word_window[:].bitcast(U32).indirect(entries))
             return both
 
-        def part(both, g):
-            apart = sbuf([P, PASSES, 2 * J], U8, f"apart{g}")
+        def part(apart, both, passes):
             nc.vector.tensor_copy(
-                out=apart[:].bitcast(U16),
-                in_=both[:].bitcast(U16).rearrange("p (j a) -> p a j", a=PASSES),
+                out=apart[:, passes, :].bitcast(U16),
+                in_=both[:].bitcast(U16).rearrange("p (j a) -> p a j", a=PASSES)[:, passes, :],
             )
-            return apart
-
-        def bank(b, name):
-            return psum.tile([P, N], F32, name=name, tag=f"bank{b}")
 
         w_codes = [sbuf([P, WIDTH], U32, f"w{a}_codes") for a in range(PASSES)]
         w_scales = [sbuf([P, WIDTH], U8, f"w{a}_scales") for a in range(PASSES)]
+        w0_bf16 = sbuf([P, WIDTH, PACK], BF16, "w0_bf16")
+        cast(w0_bf16[:], w0_raw[:])
+        quantize(w0_bf16[:], w_codes[0][:], w_scales[0][:])
 
-        def prepare_w(raw, a, cols, name):
-            grouped = sbuf([P, raw.shape[2], PACK], BF16, name)
-            cast(grouped[:], raw)
-            quantize(grouped[:], w_codes[a][:, cols], w_scales[a][:, cols])
-
-        prepare_w(w0_raw[:], 0, whole, "w0_bf16")
         iw_turned = bank(PSUM_BANKS - 1, "iw_turned")
         nc.tensor.transpose(iw_turned[:, 0:P], iw_rows[:], ident[:])
         iw_cols = sbuf([P, G * TILES], F32, "iw_cols")
         nc.scalar.copy(out=iw_cols[:], in_=iw_turned[:, 0 : G * TILES])
 
-        gathered = [look_up(0, None)]
-        picked = [part(gathered[0], 0)]
-        gathered.append(look_up(1, None))
-        picked.append(part(gathered[1], 1))
-        w1_last = sbuf([P, HALF, PACK], BF16, "w11_bf16")
-        own = HALF - W1_ON_VECTOR
-        cast(w1_last[:, own:HALF, :], w1_raw[:, :, HALF + own : WIDTH], on_vector=True)
-        prepare_w(w1_raw[:, :, halves[0]], 1, halves[0], "w10_bf16")
-        cast(w1_last[:, 0:own, :], w1_raw[:, :, HALF : HALF + own])
-        quantize(w1_last[:], w_codes[1][:, halves[1]], w_scales[1][:, halves[1]])
-        gathered.append(look_up(2, "scale_window"))
-        picked.append(part(gathered[2], 2))
+        picked = [sbuf([P, PASSES, 2 * J], U8, f"apart{g}") for g in range(G)]
+        gathered = [look_up(g) for g in range(G - 1)]
+        for a in range(PASSES):
+            for g in range(G - 1):
+                part(picked[g], gathered[g], slice(a, a + 1))
+
+        w11_bf16 = sbuf([P, HALF, PACK], BF16, "w11_bf16")
+        on_scalar = HALF - W1_ON_VECTOR
+        cast(w11_bf16[:, on_scalar:HALF, :], w1_raw[:, :, HALF + on_scalar : WIDTH], on_vector=True)
+        w10_bf16 = sbuf([P, HALF, PACK], BF16, "w10_bf16")
+        cast(w10_bf16[:], w1_raw[:, :, halves[0]])
+        quantize(w10_bf16[:], w_codes[1][:, halves[0]], w_scales[1][:, halves[0]])
+        cast(w11_bf16[:, 0:on_scalar, :], w1_raw[:, :, HALF : HALF + on_scalar])
+        quantize(w11_bf16[:], w_codes[1][:, halves[1]], w_scales[1][:, halves[1]])
+        gathered.append(look_up(G - 1, "scale_window"))
+        part(picked[G - 1], gathered[G - 1], slice(0, PASSES))
 
         tab_scale_bytes = [t[:].bitcast(U8) for t in tab_scale]
         for b, width in enumerate(WARM_UP_WIDTHS):
@@ -185,87 +179,84 @@ def tile_list_interp_none_kernel(
                 out=idle[:, 0:width],
                 lhsT=w_codes[0][:, 0:P].bitcast(FP8X4),
                 lhsT_scale=w_scales[0][:, 0:P],
-                rhs=word_window[:].bitcast(U8)[:, 0 : 2 * width].bitcast(FP4X4),
+                rhs=gathered[0][:].bitcast(U8)[:, 0 : 2 * width].bitcast(FP4X4),
                 rhs_scale=tab_scale_bytes[0][:, 0:width],
                 start=True,
                 stop=True,
             )
 
-        def look_up_pass(acc, g, jt, a, first=0):
+        def look_up_pass(acc, g, jt, a, opens=0):
             nc.tensor.matmul_mx(
                 out=acc[:],
                 lhsT=picked[g][:, a, 2 * P * jt : 2 * P * (jt + 1)].bitcast(FP4X4),
                 lhsT_scale=tab_scale_bytes[a][:, g * J + P * jt : g * J + P * (jt + 1)],
                 rhs=w_codes[a][:].bitcast(FP8X4),
                 rhs_scale=w_scales[a][:],
-                start=(a == first),
-                stop=(a != first),
+                start=(a == opens),
+                stop=(a != opens),
             )
 
-        partial = [None] * TILES
-        spare = {}
+        def weight(g, jt):
+            return iw_cols[:, TILES * g + jt : TILES * g + jt + 1]
 
-        def weigh(acc, g, jt, tag=None):
-            weight = iw_cols[:, TILES * g + jt : TILES * g + jt + 1]
-            if g == 0 or (g == 1 and jt in SPLIT_TILES):
-                total = terms[:, jt if g == 0 else TILES + SPLIT_TILES.index(jt), :]
-                nc.scalar.activation(out=total, in_=acc[:], func=COPY, scale=weight)
-                if g == 1:
-                    spare[jt] = partial[jt]
-            else:
-                total = sbuf([P, N], F32, f"partial{g}_{jt}", tag)[:]
-                nc.vector.scalar_tensor_tensor(
-                    out=total, in0=acc[:], scalar=weight, in1=partial[jt], op0=MULT, op1=ADD
-                )
-            partial[jt] = total
+        def weigh(term, acc, g, jt):
+            nc.scalar.activation(out=term, in_=acc[:], func=COPY, scale=weight(g, jt))
+            return term
 
-        x_first = sbuf([P, HALF, PACK], BF16, "x_first")
-        cast(x_first[:], x_raw[0, 0][:])
-        terms = sbuf([P, TILES + len(SPLIT_TILES), N], F32, "terms", "x00_raw")
+        def weigh_and_add(so_far, acc, g, jt, tag=None):
+            total = sbuf([P, N], F32, f"partial{g}_{jt}", tag)
+            nc.vector.scalar_tensor_tensor(
+                out=total[:], in0=acc[:], scalar=weight(g, jt), in1=so_far, op0=MULT, op1=ADD
+            )
+            return total[:]
+
+        x00_bf16 = sbuf([P, HALF, PACK], BF16, "x00_bf16")
+        cast(x00_bf16[:], x_raw[0, 0][:])
+        terms = sbuf([P, TILES + 1, N], F32, "terms", "x00_raw")
+
         early = {}
         for g in range(G - 1):
             for jt in range(TILES):
                 early[g, jt] = bank(TILES * g + jt, f"sum{g}_{jt}")
-                if TILES * g + jt < OPENED_EARLY:
+                if (g, jt) != (1, LAST_TILE):
                     look_up_pass(early[g, jt], g, jt, 0)
+        partial = []
         for jt in range(TILES):
-            for g in range(G - 1):
-                if TILES * g + jt < OPENED_EARLY:
-                    look_up_pass(early[g, jt], g, jt, 1)
-                    weigh(early[g, jt], g, jt)
-        for late in reversed(range(OPENED_EARLY, PSUM_BANKS)):
-            g, jt = divmod(late, TILES)
-            for a in (1, 0):
-                look_up_pass(early[g, jt], g, jt, a, first=1)
-            weigh(early[g, jt], g, jt)
+            look_up_pass(early[0, jt], 0, jt, 1)
+            partial.append(weigh(terms[:, jt, :], early[0, jt], 0, jt))
+            if jt != LAST_TILE:
+                look_up_pass(early[1, jt], 1, jt, 1)
+                partial[jt] = weigh_and_add(partial[jt], early[1, jt], 1, jt)
+        for a in reversed(range(PASSES)):
+            look_up_pass(early[1, LAST_TILE], 1, LAST_TILE, a, opens=1)
+        first_term = partial[LAST_TILE]
+        partial[LAST_TILE] = weigh(terms[:, TILES, :], early[1, LAST_TILE], 1, LAST_TILE)
 
-        codes = [sbuf([P, PASSES * HALF], U32, f"x_codes{h}") for h in range(HALVES)]
-        scales = [sbuf([P, PASSES * HALF], U8, f"x{h}_scales") for h in range(HALVES)]
-        quantize(x_first[:], codes[0][:, halves[0]], scales[0][:, halves[0]])
-        x_second = sbuf([P, HALF, PACK], BF16, "x_second", "apart1")
-        cast(x_second[:], x_raw[1, 0][:])
-        x_rest = sbuf([P, PASSES * HALF, PACK], BF16, "x_rest", "x_first")
+        x_codes = [sbuf([P, PASSES * HALF], U32, f"x_codes{h}") for h in range(HALVES)]
+        x_scales = [sbuf([P, PASSES * HALF], U8, f"x{h}_scales") for h in range(HALVES)]
+        quantize(x00_bf16[:], x_codes[0][:, halves[0]], x_scales[0][:, halves[0]])
+        x10_bf16 = sbuf([P, HALF, PACK], BF16, "x10_bf16", "apart1")
+        cast(x10_bf16[:], x_raw[1, 0][:])
+        late_bf16 = sbuf([P, PASSES * HALF, PACK], BF16, "late_bf16", "x00_bf16")
         for a in range(PASSES):
             nc.gpsimd.tensor_scalar(
-                x_rest[:, halves[a], :],
+                late_bf16[:, halves[a], :],
                 x_raw[a, 1][:].rearrange("p i c -> p c i"),
                 1.0,
                 0.0,
                 op0=MULT,
                 op1=ADD,
             )
-        for jt, tag in enumerate((None, None, "partial1_0", "partial1_1")):
-            acc = bank(jt % (TILES - 1), f"sum2_{jt}")
+
+        for jt in range(TILES):
+            acc = bank(jt % LAST_TILE, f"sum2_{jt}")
             for a in range(PASSES):
                 look_up_pass(acc, G - 1, jt, a)
-            weigh(acc, G - 1, jt, tag)
+            tag = f"partial1_{jt - HALVES}" if jt >= HALVES else None
+            partial[jt] = weigh_and_add(partial[jt], acc, G - 1, jt, tag)
 
-        quantize(x_second[:], codes[0][:, halves[1]], scales[0][:, halves[1]])
-        quantize(x_rest[:], codes[1][:], scales[1][:])
-        xq = {}
-        for h in range(HALVES):
-            for a in range(PASSES):
-                xq[a, h] = (codes[h][:, halves[a]], scales[h][:, halves[a]])
+        quantize(x10_bf16[:], x_codes[0][:, halves[1]], x_scales[0][:, halves[1]])
+        quantize(late_bf16[:], x_codes[1][:], x_scales[1][:])
 
         pieces = [(h, u) for h in range(HALVES) for u in range(HALVES)]
 
@@ -273,22 +264,19 @@ def tile_list_interp_none_kernel(
             return t[:].rearrange("p (t j) -> p t j", t=HALVES)
 
         turned = {piece: bank(TILES + b, f"turned{b}") for b, piece in enumerate(pieces)}
-        sources = [(jt, spare[jt]) for jt in SPLIT_TILES] + list(enumerate(partial))
-        todo = {piece: HALVES * len([1 for jt, s in sources if jt // HALVES == piece[0]]) for piece in pieces}
-        done = {piece: 0 for piece in pieces}
-        for jt, source in sources:
+        sources = [(LAST_TILE, first_term)] + list(enumerate(partial))
+        for n, (jt, source) in enumerate(sources):
             h, first = jt // HALVES, P * (jt % HALVES)
+            same_half = [m for m, (other, unused) in enumerate(sources) if other // HALVES == h]
             for nt in range(TILES):
-                piece = (h, nt // HALVES)
                 nc.tensor.matmul(
-                    by_tile(turned[piece])[:, nt % HALVES, first : first + P],
+                    by_tile(turned[h, nt // HALVES])[:, nt % HALVES, first : first + P],
                     source[:, P * nt : P * (nt + 1)],
                     ident[:],
                     is_transpose=True,
-                    start=(done[piece] == 0),
-                    stop=(done[piece] == todo[piece] - 1),
+                    start=(n == same_half[0] and nt % HALVES == 0),
+                    stop=(n == same_half[-1] and nt % HALVES == HALVES - 1),
                 )
-                done[piece] = done[piece] + 1
         interpolated = {}
         for b, piece in enumerate(pieces):
             interpolated[piece] = sbuf([P, N], F32, f"interpolated{b}")
@@ -296,7 +284,7 @@ def tile_list_interp_none_kernel(
 
         wx_scale_bytes = wx_scale[:].bitcast(U8)
         for b, (h, u) in enumerate(pieces):
-            dense = bank((b - 1) % TILES if b < 1 else b % (TILES - 1), f"dense{b}")
+            dense = bank(LAST_TILE if b == 0 else b % LAST_TILE, f"dense{b}")
             for t in range(HALVES):
                 nt = HALVES * u + t
                 for a in range(PASSES):
@@ -304,12 +292,12 @@ def tile_list_interp_none_kernel(
                         out=by_tile(dense)[:, t, :],
                         lhsT=wx_word[:, a, P * nt : P * (nt + 1)].bitcast(FP8X4),
                         lhsT_scale=wx_scale_bytes[:, a, P * nt : P * (nt + 1)],
-                        rhs=xq[a, h][0].bitcast(FP8X4),
-                        rhs_scale=xq[a, h][1],
+                        rhs=x_codes[h][:, halves[a]].bitcast(FP8X4),
+                        rhs_scale=x_scales[h][:, halves[a]],
                         start=(a == 0),
                         stop=(a == PASSES - 1),
                     )
-            result = sbuf([P, J], F32, f"result{b}")
+            result = sbuf([P, N], F32, f"result{b}")
             nc.vector.tensor_tensor(
                 out=result[:], in0=dense[:], in1=interpolated[h, u][:], op=ADD
             )

@@ -29,13 +29,10 @@ WIDTH = 512
 HALVES = 2
 HALF = WIDTH // HALVES
 TILES = 4
-LAST_TILE = TILES - 1
 ROWS_A_QUAD = 4
 FIRST_ROW = P - QUAD
+IW_ROW = P - G * TILES
 LIST_COLUMNS = J // 16
-PSUM_BANKS = 8
-WARM_UP_WIDTHS = (512, 256, 256, 256)
-W1_ON_VECTOR = 128
 
 
 def tile_list_interp_none_kernel(
@@ -45,10 +42,14 @@ def tile_list_interp_none_kernel(
     with ExitStack() as ctx:
         lists = ctx.enter_context(tc.tile_pool(name="lists", bufs=1))
         keep = ctx.enter_context(tc.tile_pool(name="keep", bufs=1))
+        shared = ctx.enter_context(tc.tile_pool(name="shared", bufs=1))
         psum = ctx.enter_context(tc.psum_pool(name="psum", bufs=1))
 
         def sbuf(shape, dtype, name, tag=None):
             return keep.tile(shape, dtype, name=name, tag=tag or name, align_bytes=64)
+
+        def placed(shape, dtype, name, offset):
+            return shared.tile(shape, dtype, name=name, offset=offset, align_bytes=64)
 
         def bank(b, name):
             return psum.tile([P, N], F32, name=name, tag=f"bank{b}")
@@ -56,74 +57,85 @@ def tile_list_interp_none_kernel(
         scale_window = sbuf([P, T // 4], I32, "scale_window")
         nc.vector.memset(scale_window[0:FIRST_ROW, :], 0)
         iw_rows = sbuf([P, P], F32, "iw_rows")
-        nc.gpsimd.memset(iw_rows[:], 0.0)
-        tab_scale = [sbuf([P, G * J // 4], I32, f"tab_scale{a}") for a in range(PASSES)]
-        for a in range(PASSES):
-            nc.vector.memset(tab_scale[a][:], 0)
+        nc.gpsimd.memset(iw_rows[0:FIRST_ROW, :], 0.0)
+        nc.gpsimd.memset(iw_rows[FIRST_ROW:IW_ROW, :], 0.0)
+        tab_scale = sbuf([P, PASSES, G * J // 4], I32, "tab_scale")
+        nc.vector.memset(tab_scale[:], 0)
         wx_scale = sbuf([P, PASSES, N // 4], I32, "wx_scale")
         nc.vector.memset(wx_scale[:], 0)
         ident = sbuf([P, P], F32, "ident")
         make_identity(nc, ident[:])
 
-        whole = slice(0, WIDTH)
         halves = [slice(0, HALF), slice(HALF, WIDTH)]
 
-        def load(src, a, cols, name, tag=None):
-            raw = sbuf([P, PACK, cols.stop - cols.start], F32, name, tag)
+        def load(src, a, cols, name, offset=None):
+            if offset is None:
+                raw = sbuf([P, PACK, cols.stop - cols.start], F32, name)
+            else:
+                raw = placed([P, PACK, cols.stop - cols.start], F32, name, offset)
             rows = src[a * K_PASS : (a + 1) * K_PASS, cols]
             nc.sync.dma_start(out=raw[:], in_=rows.rearrange("(p i) c -> p i c", i=PACK))
             return raw
 
         offsets = lists.tile([P, G * LIST_COLUMNS], U16, name="offsets")
         nc.sync.dma_start(offsets[:], offs)
-        nc.sync.dma_start(
-            out=scale_window[FIRST_ROW:P, :],
-            in_=tab_scales.bitcast(I32).rearrange("a s t -> (a s) t"),
-        )
-        w0_raw = load(w, 0, whole, "w0_raw")
-        for g, vec in enumerate((iw0, iw1, iw2)):
+        for a in range(PASSES):
             nc.sync.dma_start(
-                out=iw_rows[TILES * g : TILES * (g + 1), :],
+                out=scale_window[FIRST_ROW + a : P : PASSES, :],
+                in_=tab_scales[a].bitcast(I32).rearrange("(q r) t -> r q t", r=ROWS_A_QUAD),
+            )
+        for g, vec in enumerate((iw0, iw1, iw2)):
+            nc.scalar.dma_start(
+                out=iw_rows[IW_ROW + TILES * g : IW_ROW + TILES * (g + 1), :],
                 in_=vec.rearrange("(c p) -> c p", p=P),
             )
         word_window = sbuf([P, T], I32, "word_window")
         nc.sync.dma_start(
             out=word_window[:], in_=tab_words[0].rearrange("p t b -> p (t b)").bitcast(I32)
         )
+        quarters = [slice(0, P), slice(P, HALF)]
+        w_first = [load(w, 0, cols, f"w00{u}_raw") for u, cols in enumerate(quarters)]
+        w_raw = {}
+        w_raw[1, 0] = load(w, 1, halves[0], "w10_raw", 0)
 
         picked_scales = sbuf([P, G * J], U8, "picked_scales")
         nc.vector.tensor_copy(picked_scales[:], scale_window[:].bitcast(U8).indirect(offsets[:]))
-
-        def place_scales(a):
-            first = FIRST_ROW + a * QUADS * ROWS_A_QUAD
-            for r in range(ROWS_A_QUAD):
-                rows = slice(first + r, first + QUADS * ROWS_A_QUAD, ROWS_A_QUAD)
-                nc.sync.dma_start(
-                    out=tab_scale[a][r:P:QUAD, :], in_=picked_scales[rows, :].bitcast(I32)
-                )
-
-        place_scales(0)
-        w1_raw = load(w, 1, whole, "w1_raw", "scale_window")
-        place_scales(1)
+        for r in range(ROWS_A_QUAD):
+            first = FIRST_ROW + QUADS * PASSES * r
+            nc.sync.dma_start(
+                out=tab_scale[r:P:QUAD, :, :],
+                in_=picked_scales[first : first + QUADS * PASSES, :].bitcast(I32),
+            )
+        for a in range(PASSES):
+            w_raw[a, 1] = load(w, a, halves[1], f"w{a}1_raw")
         x_raw = {}
         for h in range(HALVES):
-            for a in range(PASSES):
-                x_raw[a, h] = load(x, a, halves[h], f"x{a}{h}_raw")
+            x_raw[0, h] = load(x, 0, halves[h], f"x0{h}_raw")
+        x1_raw = placed([P, HALVES, PACK, HALF], F32, "x1_raw", 4096)
+
+        def load_x1(h):
+            rows = x[K_PASS:L, halves[h]]
+            nc.sync.dma_start(out=x1_raw[:, h], in_=rows.rearrange("(p i) c -> p i c", i=PACK))
+
+        load_x1(0)
+        wx_scale_rows = wx_scales.bitcast(I32).rearrange("a (q r) n -> r q a n", r=ROWS_A_QUAD)
+        for r in range(ROWS_A_QUAD):
+            nc.sync.dma_start(out=wx_scale[r:P:QUAD, :, :], in_=wx_scale_rows[r])
+        load_x1(1)
         wx_word = sbuf([P, PASSES, N], I32, "wx_word")
         nc.sync.dma_start(
             out=wx_word[:], in_=wx_words.rearrange("a p n b -> p a (n b)").bitcast(I32)
         )
-        wx_scale_rows = wx_scales.bitcast(I32).rearrange("a (q r) n -> r q a n", r=ROWS_A_QUAD)
-        for r in range(ROWS_A_QUAD):
-            nc.sync.dma_start(out=wx_scale[r:P:QUAD, :, :], in_=wx_scale_rows[r])
 
-        def cast(grouped, raw, on_vector=False):
+        def cast(grouped, raw):
             target = grouped.rearrange("p (c u) i -> p c i u", u=4)
             source = raw.rearrange("p i (c u) -> p c i u", u=4)
-            if on_vector:
-                nc.vector.tensor_copy(out=target, in_=source)
-            else:
-                nc.scalar.activation(out=target, in_=source, func=COPY)
+            nc.scalar.activation(out=target, in_=source, func=COPY)
+
+        def cast_on_gpsimd(grouped, raw):
+            nc.gpsimd.tensor_scalar(
+                grouped, raw.rearrange("p i c -> p c i"), 1.0, 0.0, op0=MULT, op1=ADD
+            )
 
         def quantize(grouped, codes, scales):
             nc.vector.quantize_mx(
@@ -132,174 +144,189 @@ def tile_list_interp_none_kernel(
                 in_=grouped.rearrange("p c i -> p (c i)"),
             )
 
-        def look_up(g, tag=None):
-            both = sbuf([P, J], U32, f"both{g}", tag)
-            entries = offsets[:, g * LIST_COLUMNS : (g + 1) * LIST_COLUMNS]
+        def look_up(run, both):
+            entries = offsets[:, run.start * P // 16 : run.stop * P // 16]
             nc.vector.tensor_copy(both[:], word_window[:].bitcast(U32).indirect(entries))
             return both
 
-        def part(apart, both, passes):
+        picked = {}
+
+        def part(run, apart, both):
             nc.vector.tensor_copy(
-                out=apart[:, passes, :].bitcast(U16),
-                in_=both[:].bitcast(U16).rearrange("p (j a) -> p a j", a=PASSES)[:, passes, :],
+                out=apart.bitcast(U16),
+                in_=both[:].bitcast(U16).rearrange("p (j a) -> p a j", a=PASSES),
             )
+            for m in run:
+                picked[m] = apart[:, :, 2 * P * (m - run.start) : 2 * P * (m - run.start + 1)]
 
-        w_codes = [sbuf([P, WIDTH], U32, f"w{a}_codes") for a in range(PASSES)]
-        w_scales = [sbuf([P, WIDTH], U8, f"w{a}_scales") for a in range(PASSES)]
-        w0_bf16 = sbuf([P, WIDTH, PACK], BF16, "w0_bf16")
-        cast(w0_bf16[:], w0_raw[:])
-        quantize(w0_bf16[:], w_codes[0][:], w_scales[0][:])
-
-        iw_turned = bank(PSUM_BANKS - 1, "iw_turned")
+        iw_turned = bank(7, "iw_turned")
         nc.tensor.transpose(iw_turned[:, 0:P], iw_rows[:], ident[:])
-        iw_cols = sbuf([P, G * TILES], F32, "iw_cols")
-        nc.scalar.copy(out=iw_cols[:], in_=iw_turned[:, 0 : G * TILES])
 
-        picked = [sbuf([P, PASSES, 2 * J], U8, f"apart{g}") for g in range(G)]
-        gathered = [look_up(g) for g in range(G - 1)]
+        w_codes, w_scales = {}, {}
+        runs = [range(0, 5), range(5, 8), range(8, 12)]
+        rounded = [sbuf([P, HALF, PACK], BF16, f"w{a}0_bf16") for a in range(PASSES)]
         for a in range(PASSES):
-            for g in range(G - 1):
-                part(picked[g], gathered[g], slice(a, a + 1))
+            w_codes[a, 0] = sbuf([P, HALF], U32, f"w{a}0_codes")[:]
+            w_scales[a, 0] = sbuf([P, HALF], U8, f"w{a}0_scales")[:]
 
-        w11_bf16 = sbuf([P, HALF, PACK], BF16, "w11_bf16")
-        on_scalar = HALF - W1_ON_VECTOR
-        cast(w11_bf16[:, on_scalar:HALF, :], w1_raw[:, :, HALF + on_scalar : WIDTH], on_vector=True)
-        w10_bf16 = sbuf([P, HALF, PACK], BF16, "w10_bf16")
-        cast(w10_bf16[:], w1_raw[:, :, halves[0]])
-        quantize(w10_bf16[:], w_codes[1][:, halves[0]], w_scales[1][:, halves[0]])
-        cast(w11_bf16[:, 0:on_scalar, :], w1_raw[:, :, HALF : HALF + on_scalar])
-        quantize(w11_bf16[:], w_codes[1][:, halves[1]], w_scales[1][:, halves[1]])
-        gathered.append(look_up(G - 1, "scale_window"))
-        part(picked[G - 1], gathered[G - 1], slice(0, PASSES))
+        def prepare(a, cols, raw):
+            cast(rounded[a][:, cols, :], raw[:])
+            quantize(rounded[a][:, cols, :], w_codes[a, 0][:, cols], w_scales[a, 0][:, cols])
 
-        tab_scale_bytes = [t[:].bitcast(U8) for t in tab_scale]
-        for b, width in enumerate(WARM_UP_WIDTHS):
+        gathered = [look_up(runs[0], sbuf([P, P * len(runs[0])], U32, "both0"))]
+        prepare(0, quarters[0], w_first[0])
+        gathered.append(look_up(runs[1], sbuf([P, P * len(runs[1])], U32, "both1", "w000_raw")))
+        prepare(0, quarters[1], w_first[1])
+        early = sbuf([P, 4 * P * runs[1].stop], U8, "early_apart", "w001_raw")
+        for run, both in zip(runs, gathered):
+            apart = early[:, 4 * P * run.start : 4 * P * run.stop]
+            part(run, apart.rearrange("p (a b) -> p a b", a=PASSES), both)
+        prepare(1, halves[0], w_raw[1, 0])
+        iw_cols = placed([P, G * TILES], F32, "iw_cols", 4 * J)
+        nc.scalar.copy(out=iw_cols[:], in_=iw_turned[:, IW_ROW:P])
+        for b, width in enumerate((512, 512, 512)):
             idle = bank(b, f"idle{b}")
             nc.tensor.matmul_mx(
                 out=idle[:, 0:width],
-                lhsT=w_codes[0][:, 0:P].bitcast(FP8X4),
-                lhsT_scale=w_scales[0][:, 0:P],
+                lhsT=w_codes[0, 0][:, 0:P].bitcast(FP8X4),
+                lhsT_scale=w_scales[0, 0][:, 0:P],
                 rhs=gathered[0][:].bitcast(U8)[:, 0 : 2 * width].bitcast(FP4X4),
-                rhs_scale=tab_scale_bytes[0][:, 0:width],
+                rhs_scale=picked_scales[:, 0:width],
                 start=True,
                 stop=True,
             )
+        both2 = look_up(runs[2], placed([P, J], U32, "both2", 0))
+        late_w = sbuf([P, WIDTH, PACK], BF16, "late_w")
+        late_codes = sbuf([P, WIDTH], U32, "late_codes")
+        late_scales = sbuf([P, WIDTH], U8, "late_scales")
+        for a in range(PASSES):
+            cast(late_w[:, halves[a], :], w_raw[a, 1][:])
+            w_codes[a, 1], w_scales[a, 1] = late_codes[:, halves[a]], late_scales[:, halves[a]]
+            quantize(late_w[:, halves[a], :], w_codes[a, 1], w_scales[a, 1])
+            if a == 0:
+                late_apart = sbuf([P, PASSES, 2 * J], U8, "late_apart", "w01_raw")
+                part(runs[2], late_apart[:], both2)
 
-        def look_up_pass(acc, g, jt, a, opens=0):
-            nc.tensor.matmul_mx(
-                out=acc[:],
-                lhsT=picked[g][:, a, 2 * P * jt : 2 * P * (jt + 1)].bitcast(FP4X4),
-                lhsT_scale=tab_scale_bytes[a][:, g * J + P * jt : g * J + P * (jt + 1)],
-                rhs=w_codes[a][:].bitcast(FP8X4),
-                rhs_scale=w_scales[a][:],
-                start=(a == opens),
-                stop=(a != opens),
-            )
+        tab_scale_bytes = tab_scale[:].bitcast(U8)
+
+        def look_up_passes(banks, g, h, a):
+            for jt in range(TILES):
+                nc.tensor.matmul_mx(
+                    out=banks[jt // 2][:, halves[jt % 2]],
+                    lhsT=picked[TILES * g + jt][:, a, :].bitcast(FP4X4),
+                    lhsT_scale=tab_scale_bytes[:, a, g * J + P * jt : g * J + P * (jt + 1)],
+                    rhs=w_codes[a, h].bitcast(FP8X4),
+                    rhs_scale=w_scales[a, h],
+                    start=(a == 0 and jt % 2 == 0),
+                    stop=(a == PASSES - 1 and jt % 2 == 1),
+                )
+
+        def pair(first, name):
+            return [bank(first + u, f"{name}_{u}") for u in range(2)]
 
         def weight(g, jt):
             return iw_cols[:, TILES * g + jt : TILES * g + jt + 1]
 
-        def weigh(term, acc, g, jt):
-            nc.scalar.activation(out=term, in_=acc[:], func=COPY, scale=weight(g, jt))
-            return term
-
-        def weigh_and_add(so_far, acc, g, jt, tag=None):
-            total = sbuf([P, N], F32, f"partial{g}_{jt}", tag)
-            nc.vector.scalar_tensor_tensor(
-                out=total[:], in0=acc[:], scalar=weight(g, jt), in1=so_far, op0=MULT, op1=ADD
-            )
-            return total[:]
-
-        x00_bf16 = sbuf([P, HALF, PACK], BF16, "x00_bf16")
-        cast(x00_bf16[:], x_raw[0, 0][:])
-        terms = sbuf([P, TILES + 1, N], F32, "terms", "x00_raw")
-
-        early = {}
-        for g in range(G - 1):
+        def weigh(terms, banks, g):
             for jt in range(TILES):
-                early[g, jt] = bank(TILES * g + jt, f"sum{g}_{jt}")
-                if (g, jt) != (1, LAST_TILE):
-                    look_up_pass(early[g, jt], g, jt, 0)
-        partial = []
-        for jt in range(TILES):
-            look_up_pass(early[0, jt], 0, jt, 1)
-            partial.append(weigh(terms[:, jt, :], early[0, jt], 0, jt))
-            if jt != LAST_TILE:
-                look_up_pass(early[1, jt], 1, jt, 1)
-                partial[jt] = weigh_and_add(partial[jt], early[1, jt], 1, jt)
-        for a in reversed(range(PASSES)):
-            look_up_pass(early[1, LAST_TILE], 1, LAST_TILE, a, opens=1)
-        first_term = partial[LAST_TILE]
-        partial[LAST_TILE] = weigh(terms[:, TILES, :], early[1, LAST_TILE], 1, LAST_TILE)
-
-        x_codes = [sbuf([P, PASSES * HALF], U32, f"x_codes{h}") for h in range(HALVES)]
-        x_scales = [sbuf([P, PASSES * HALF], U8, f"x{h}_scales") for h in range(HALVES)]
-        quantize(x00_bf16[:], x_codes[0][:, halves[0]], x_scales[0][:, halves[0]])
-        x10_bf16 = sbuf([P, HALF, PACK], BF16, "x10_bf16", "apart1")
-        cast(x10_bf16[:], x_raw[1, 0][:])
-        late_bf16 = sbuf([P, PASSES * HALF, PACK], BF16, "late_bf16", "x00_bf16")
-        for a in range(PASSES):
-            nc.gpsimd.tensor_scalar(
-                late_bf16[:, halves[a], :],
-                x_raw[a, 1][:].rearrange("p i c -> p c i"),
-                1.0,
-                0.0,
-                op0=MULT,
-                op1=ADD,
-            )
-
-        for jt in range(TILES):
-            acc = bank(jt % LAST_TILE, f"sum2_{jt}")
-            for a in range(PASSES):
-                look_up_pass(acc, G - 1, jt, a)
-            tag = f"partial1_{jt - HALVES}" if jt >= HALVES else None
-            partial[jt] = weigh_and_add(partial[jt], acc, G - 1, jt, tag)
-
-        quantize(x10_bf16[:], x_codes[0][:, halves[1]], x_scales[0][:, halves[1]])
-        quantize(late_bf16[:], x_codes[1][:], x_scales[1][:])
-
-        pieces = [(h, u) for h in range(HALVES) for u in range(HALVES)]
-
-        def by_tile(t):
-            return t[:].rearrange("p (t j) -> p t j", t=HALVES)
-
-        turned = {piece: bank(TILES + b, f"turned{b}") for b, piece in enumerate(pieces)}
-        sources = [(LAST_TILE, first_term)] + list(enumerate(partial))
-        for n, (jt, source) in enumerate(sources):
-            h, first = jt // HALVES, P * (jt % HALVES)
-            same_half = [m for m, (other, unused) in enumerate(sources) if other // HALVES == h]
-            for nt in range(TILES):
-                nc.tensor.matmul(
-                    by_tile(turned[h, nt // HALVES])[:, nt % HALVES, first : first + P],
-                    source[:, P * nt : P * (nt + 1)],
-                    ident[:],
-                    is_transpose=True,
-                    start=(n == same_half[0] and nt % HALVES == 0),
-                    stop=(n == same_half[-1] and nt % HALVES == HALVES - 1),
+                nc.scalar.activation(
+                    out=terms[:, jt, :],
+                    in_=banks[jt // 2][:, halves[jt % 2]],
+                    func=COPY,
+                    scale=weight(g, jt),
                 )
-        interpolated = {}
-        for b, piece in enumerate(pieces):
-            interpolated[piece] = sbuf([P, N], F32, f"interpolated{b}")
-            nc.scalar.copy(out=interpolated[piece][:], in_=turned[piece][:])
+
+        def weigh_and_add(total, so_far, banks, g):
+            for jt in range(TILES):
+                nc.vector.scalar_tensor_tensor(
+                    out=total[:, jt, :],
+                    in0=banks[jt // 2][:, halves[jt % 2]],
+                    scalar=weight(g, jt),
+                    in1=so_far[:, jt, :],
+                    op0=MULT,
+                    op1=ADD,
+                )
+
+        def turn(banks, total):
+            for t in range(2):
+                for jt in range(TILES):
+                    nc.tensor.matmul(
+                        banks[t][:, P * jt : P * (jt + 1)],
+                        total[:, jt, P * t : P * (t + 1)],
+                        ident[:],
+                        is_transpose=True,
+                        start=(jt == 0),
+                        stop=(jt == TILES - 1),
+                    )
+
+        sums = {(g, 0): pair(2 * g, f"sum{g}0") for g in range(G)}
+        for a in range(PASSES):
+            for g in range(G - 1):
+                look_up_passes(sums[g, 0], g, 0, a)
+        for a in range(PASSES):
+            look_up_passes(sums[2, 0], 2, 0, a)
+        terms_a = sbuf([P, TILES, HALF], F32, "terms_a", "w11_raw")
+        weigh(terms_a[:], sums[0, 0], 0)
+        two_a = sbuf([P, TILES, HALF], F32, "two_a")
+        weigh_and_add(two_a[:], terms_a[:], sums[1, 0], 1)
+        three_a = sbuf([P, TILES, HALF], F32, "three_a")
+        weigh_and_add(three_a[:], two_a[:], sums[2, 0], 2)
+
+        x_bf16 = [
+            sbuf([P, WIDTH, PACK], BF16, "x0_bf16", "late_w"),
+            sbuf([P, WIDTH, PACK], BF16, "x1_bf16"),
+        ]
+        x_codes = [sbuf([P, WIDTH], U32, f"x{a}_codes") for a in range(PASSES)]
+        x_scales = [sbuf([P, WIDTH], U8, f"x{a}_scales") for a in range(PASSES)]
+        cast_on_gpsimd(x_bf16[0][:, halves[0], :], x_raw[0, 0][:])
+        cast(x_bf16[0][:, halves[1], :], x_raw[0, 1][:])
+        quantize(x_bf16[0][:], x_codes[0][:], x_scales[0][:])
+
+        for g, first in enumerate((6, 0, 2)):
+            sums[g, 1] = pair(first, f"sum{g}1")
+            for a in range(PASSES):
+                look_up_passes(sums[g, 1], g, 1, a)
+        terms_b = sbuf([P, TILES, HALF], F32, "terms_b", "x01_raw")
+        weigh(terms_b[:], sums[0, 1], 0)
+        two_b = sbuf([P, TILES, HALF], F32, "two_b")
+        weigh_and_add(two_b[:], terms_b[:], sums[1, 1], 1)
+
+        cast_on_gpsimd(x_bf16[1][:, halves[0], :], x1_raw[:, 0])
+        cast_on_gpsimd(x_bf16[1][:, HALF : HALF + P, :], x1_raw[:, 1, :, 0:P])
+        cast(x_bf16[1][:, HALF + P : WIDTH, :], x1_raw[:, 1, :, P:HALF])
+        quantize(x_bf16[1][:], x_codes[1][:], x_scales[1][:])
+        late = placed([P, 2, TILES, HALF], F32, "late", 8192)
+        three_b = late[:, 0]
+        weigh_and_add(three_b, two_b[:], sums[2, 1], 2)
+
+        turned_a = pair(4, "turned_a")
+        turn(turned_a, three_a[:])
+        held = []
+        for t in range(2):
+            held.append(late[:, 1, 2 * t : 2 * t + 2, :].rearrange("p c j -> p (c j)"))
+            nc.scalar.copy(out=held[t], in_=turned_a[t][:])
 
         wx_scale_bytes = wx_scale[:].bitcast(U8)
-        for b, (h, u) in enumerate(pieces):
-            dense = bank(LAST_TILE if b == 0 else b % LAST_TILE, f"dense{b}")
-            for t in range(HALVES):
-                nt = HALVES * u + t
-                for a in range(PASSES):
-                    nc.tensor.matmul_mx(
-                        out=by_tile(dense)[:, t, :],
-                        lhsT=wx_word[:, a, P * nt : P * (nt + 1)].bitcast(FP8X4),
-                        lhsT_scale=wx_scale_bytes[:, a, P * nt : P * (nt + 1)],
-                        rhs=x_codes[h][:, halves[a]].bitcast(FP8X4),
-                        rhs_scale=x_scales[h][:, halves[a]],
-                        start=(a == 0),
-                        stop=(a == PASSES - 1),
-                    )
-            result = sbuf([P, N], F32, f"result{b}")
-            nc.vector.tensor_tensor(
-                out=result[:], in0=dense[:], in1=interpolated[h, u][:], op=ADD
-            )
-            rows = out[HALVES * P * u : HALVES * P * (u + 1), halves[h]]
-            nc.sync.dma_start(out=rows.rearrange("(t p) j -> p t j", p=P), in_=by_tile(result))
+        dense = pair(6, "dense_a") + pair(0, "dense_b")
+        for nt in (0, 2, 3, 1):
+            for a in range(PASSES):
+                nc.tensor.matmul_mx(
+                    out=dense[nt][:],
+                    lhsT=wx_word[:, a, P * nt : P * (nt + 1)].bitcast(FP8X4),
+                    lhsT_scale=wx_scale_bytes[:, a, P * nt : P * (nt + 1)],
+                    rhs=x_codes[a][:].bitcast(FP8X4),
+                    rhs_scale=x_scales[a][:],
+                    start=(a == 0),
+                    stop=(a == PASSES - 1),
+                )
+        for nt in range(2, TILES):
+            copied = sbuf([P, J], F32, f"dense{nt}")
+            nc.scalar.copy(out=copied[:], in_=dense[nt][:])
+            held.append(copied[:])
+        turned_b = pair(0, "turned_b")
+        turn(turned_b, three_b)
+
+        for nt, last in enumerate(dense[0:2] + turned_b):
+            result = sbuf([P, J], F32, f"result{nt}")
+            nc.vector.tensor_tensor(out=result[:], in0=last[:], in1=held[nt], op=ADD)
+            nc.sync.dma_start(out=out[P * nt : P * (nt + 1), :], in_=result[:])

@@ -108,20 +108,12 @@ def tile_list_interp_none_kernel(
             )
         for a in range(PASSES):
             w_raw[a, 1] = load(w, a, halves[1], f"w{a}1_raw")
-        x_raw = {}
-        for h in range(HALVES):
-            x_raw[0, h] = load(x, 0, halves[h], f"x0{h}_raw")
-        x1_raw = placed([P, HALVES, PACK, HALF], F32, "x1_raw", 4096)
-
-        def load_x1(h):
-            rows = x[K_PASS:L, halves[h]]
-            nc.sync.dma_start(out=x1_raw[:, h], in_=rows.rearrange("(p i) c -> p i c", i=PACK))
-
-        load_x1(0)
+        whole = slice(0, WIDTH)
+        x0_raw = load(x, 0, whole, "x0_raw")
         wx_scale_rows = wx_scales.bitcast(I32).rearrange("a (q r) n -> r q a n", r=ROWS_A_QUAD)
         for r in range(ROWS_A_QUAD):
             nc.sync.dma_start(out=wx_scale[r:P:QUAD, :, :], in_=wx_scale_rows[r])
-        load_x1(1)
+        x1_raw = load(x, 1, whole, "x1_raw", 4096)
         wx_word = sbuf([P, PASSES, N], I32, "wx_word")
         nc.sync.dma_start(
             out=wx_word[:], in_=wx_words.rearrange("a p n b -> p a (n b)").bitcast(I32)
@@ -272,29 +264,26 @@ def tile_list_interp_none_kernel(
         three_a = sbuf([P, TILES, HALF], F32, "three_a")
         weigh_and_add(three_a[:], two_a[:], sums[2, 0], 2)
 
-        x_bf16 = [
-            sbuf([P, WIDTH, PACK], BF16, "x0_bf16", "late_w"),
-            sbuf([P, WIDTH, PACK], BF16, "x1_bf16"),
-        ]
+        x0_bf16 = sbuf([P, WIDTH, PACK], BF16, "x0_bf16", "late_w")
         x_codes = [sbuf([P, WIDTH], U32, f"x{a}_codes") for a in range(PASSES)]
         x_scales = [sbuf([P, WIDTH], U8, f"x{a}_scales") for a in range(PASSES)]
-        cast_on_gpsimd(x_bf16[0][:, halves[0], :], x_raw[0, 0][:])
-        cast(x_bf16[0][:, halves[1], :], x_raw[0, 1][:])
-        quantize(x_bf16[0][:], x_codes[0][:], x_scales[0][:])
+        cast_on_gpsimd(x0_bf16[:, halves[0], :], x0_raw[:, :, halves[0]])
+        cast(x0_bf16[:, halves[1], :], x0_raw[:, :, halves[1]])
+        quantize(x0_bf16[:], x_codes[0][:], x_scales[0][:])
 
         for g, first in enumerate((6, 0, 2)):
             sums[g, 1] = pair(first, f"sum{g}1")
             for a in range(PASSES):
                 look_up_passes(sums[g, 1], g, 1, a)
-        terms_b = sbuf([P, TILES, HALF], F32, "terms_b", "x01_raw")
+        terms_b = sbuf([P, TILES, HALF], F32, "terms_b", "x0_raw")
         weigh(terms_b[:], sums[0, 1], 0)
         two_b = sbuf([P, TILES, HALF], F32, "two_b")
         weigh_and_add(two_b[:], terms_b[:], sums[1, 1], 1)
 
-        cast_on_gpsimd(x_bf16[1][:, halves[0], :], x1_raw[:, 0])
-        cast_on_gpsimd(x_bf16[1][:, HALF : HALF + P, :], x1_raw[:, 1, :, 0:P])
-        cast(x_bf16[1][:, HALF + P : WIDTH, :], x1_raw[:, 1, :, P:HALF])
-        quantize(x_bf16[1][:], x_codes[1][:], x_scales[1][:])
+        x1_bf16 = sbuf([P, WIDTH, PACK], BF16, "x1_bf16", "late_w")
+        cast_on_gpsimd(x1_bf16[:, halves[0], :], x1_raw[:, :, halves[0]])
+        cast(x1_bf16[:, halves[1], :], x1_raw[:, :, halves[1]])
+        quantize(x1_bf16[:], x_codes[1][:], x_scales[1][:])
         late = placed([P, 2, TILES, HALF], F32, "late", 8192)
         three_b = late[:, 0]
         weigh_and_add(three_b, two_b[:], sums[2, 1], 2)

@@ -59,8 +59,9 @@ def tile_list_interp_none_kernel(
         iw_rows = sbuf([P, P], F32, "iw_rows")
         nc.gpsimd.memset(iw_rows[0:FIRST_ROW, :], 0.0)
         nc.gpsimd.memset(iw_rows[FIRST_ROW:IW_ROW, :], 0.0)
-        tab_scale = sbuf([P, PASSES, G * J // 4], I32, "tab_scale")
-        nc.vector.memset(tab_scale[:], 0)
+        tab_scale = [sbuf([P, G * J // 4], I32, f"tab_scale{a}") for a in range(PASSES)]
+        for a in range(PASSES):
+            nc.vector.memset(tab_scale[a][:], 0)
         wx_scale = sbuf([P, PASSES, N // 4], I32, "wx_scale")
         nc.vector.memset(wx_scale[:], 0)
         ident = sbuf([P, P], F32, "ident")
@@ -79,13 +80,12 @@ def tile_list_interp_none_kernel(
 
         offsets = lists.tile([P, G * LIST_COLUMNS], U16, name="offsets")
         nc.sync.dma_start(offsets[:], offs)
-        for a in range(PASSES):
-            nc.sync.dma_start(
-                out=scale_window[FIRST_ROW + a : P : PASSES, :],
-                in_=tab_scales[a].bitcast(I32).rearrange("(q r) t -> r q t", r=ROWS_A_QUAD),
-            )
+        nc.sync.dma_start(
+            out=scale_window[FIRST_ROW:P, :],
+            in_=tab_scales.bitcast(I32).rearrange("a s t -> (a s) t"),
+        )
         for g, vec in enumerate((iw0, iw1, iw2)):
-            nc.scalar.dma_start(
+            nc.gpsimd.dma_start(
                 out=iw_rows[IW_ROW + TILES * g : IW_ROW + TILES * (g + 1), :],
                 in_=vec.rearrange("(c p) -> c p", p=P),
             )
@@ -93,36 +93,42 @@ def tile_list_interp_none_kernel(
         nc.sync.dma_start(
             out=word_window[:], in_=tab_words[0].rearrange("p t b -> p (t b)").bitcast(I32)
         )
-        quarters = [slice(0, P), slice(P, HALF)]
-        w_first = [load(w, 0, cols, f"w00{u}_raw") for u, cols in enumerate(quarters)]
-        w_raw = {}
-        w_raw[1, 0] = load(w, 1, halves[0], "w10_raw", 0)
-
         picked_scales = sbuf([P, G * J], U8, "picked_scales")
         nc.vector.tensor_copy(picked_scales[:], scale_window[:].bitcast(U8).indirect(offsets[:]))
-        for r in range(ROWS_A_QUAD):
-            first = FIRST_ROW + QUADS * PASSES * r
-            nc.sync.dma_start(
-                out=tab_scale[r:P:QUAD, :, :],
-                in_=picked_scales[first : first + QUADS * PASSES, :].bitcast(I32),
-            )
+
+        def place_scales(a):
+            first = FIRST_ROW + a * QUADS * ROWS_A_QUAD
+            for r in range(ROWS_A_QUAD):
+                rows = slice(first + r, first + QUADS * ROWS_A_QUAD, ROWS_A_QUAD)
+                nc.sync.dma_start(
+                    out=tab_scale[a][r:P:QUAD, :], in_=picked_scales[rows, :].bitcast(I32)
+                )
+
+        w_raw = {}
+        for a in range(PASSES):
+            w_raw[a, 0] = load(w, a, halves[0], f"w{a}0_raw", 4096 * a)
+            place_scales(a)
         for a in range(PASSES):
             w_raw[a, 1] = load(w, a, halves[1], f"w{a}1_raw")
         whole = slice(0, WIDTH)
         x0_raw = load(x, 0, whole, "x0_raw")
+        x1_raw = load(x, 1, whole, "x1_raw", 8192)
         wx_scale_rows = wx_scales.bitcast(I32).rearrange("a (q r) n -> r q a n", r=ROWS_A_QUAD)
         for r in range(ROWS_A_QUAD):
             nc.sync.dma_start(out=wx_scale[r:P:QUAD, :, :], in_=wx_scale_rows[r])
-        x1_raw = load(x, 1, whole, "x1_raw", 4096)
-        wx_word = sbuf([P, PASSES, N], I32, "wx_word")
-        nc.sync.dma_start(
-            out=wx_word[:], in_=wx_words.rearrange("a p n b -> p a (n b)").bitcast(I32)
-        )
+        wx_word = [sbuf([P, N], I32, f"wx_word{a}") for a in range(PASSES)]
+        for a in range(PASSES):
+            nc.sync.dma_start(
+                out=wx_word[a][:], in_=wx_words[a].rearrange("p n b -> p (n b)").bitcast(I32)
+            )
 
-        def cast(grouped, raw):
+        def cast(grouped, raw, on_vector=False):
             target = grouped.rearrange("p (c u) i -> p c i u", u=4)
             source = raw.rearrange("p i (c u) -> p c i u", u=4)
-            nc.scalar.activation(out=target, in_=source, func=COPY)
+            if on_vector:
+                nc.vector.tensor_copy(out=target, in_=source)
+            else:
+                nc.scalar.activation(out=target, in_=source, func=COPY)
 
         def cast_on_gpsimd(grouped, raw):
             nc.gpsimd.tensor_scalar(
@@ -155,62 +161,50 @@ def tile_list_interp_none_kernel(
         nc.tensor.transpose(iw_turned[:, 0:P], iw_rows[:], ident[:])
 
         w_codes, w_scales = {}, {}
-        runs = [range(0, 5), range(5, 8), range(8, 12)]
-        rounded = [sbuf([P, HALF, PACK], BF16, f"w{a}0_bf16") for a in range(PASSES)]
-        for a in range(PASSES):
+        runs = [range(TILES * g, TILES * (g + 1)) for g in range(G)]
+
+        def prepare(a):
+            rounded = sbuf([P, HALF, PACK], BF16, f"w{a}0_bf16")
+            cast(rounded[:], w_raw[a, 0][:])
             w_codes[a, 0] = sbuf([P, HALF], U32, f"w{a}0_codes")[:]
             w_scales[a, 0] = sbuf([P, HALF], U8, f"w{a}0_scales")[:]
+            quantize(rounded[:], w_codes[a, 0], w_scales[a, 0])
 
-        def prepare(a, cols, raw):
-            cast(rounded[a][:, cols, :], raw[:])
-            quantize(rounded[a][:, cols, :], w_codes[a, 0][:, cols], w_scales[a, 0][:, cols])
-
-        gathered = [look_up(runs[0], sbuf([P, P * len(runs[0])], U32, "both0"))]
-        prepare(0, quarters[0], w_first[0])
-        gathered.append(look_up(runs[1], sbuf([P, P * len(runs[1])], U32, "both1", "w000_raw")))
-        prepare(0, quarters[1], w_first[1])
-        early = sbuf([P, 4 * P * runs[1].stop], U8, "early_apart", "w001_raw")
-        for run, both in zip(runs, gathered):
-            apart = early[:, 4 * P * run.start : 4 * P * run.stop]
-            part(run, apart.rearrange("p (a b) -> p a b", a=PASSES), both)
-        prepare(1, halves[0], w_raw[1, 0])
-        iw_cols = placed([P, G * TILES], F32, "iw_cols", 4 * J)
+        gathered = [look_up(runs[g], sbuf([P, J], U32, f"both{g}")) for g in range(G - 1)]
+        part(runs[0], sbuf([P, PASSES, 2 * J], U8, "apart0")[:], gathered[0])
+        prepare(0)
+        part(runs[1], placed([P, PASSES, 2 * J], U8, "apart1", 0)[:], gathered[1])
+        gathered.append(look_up(runs[2], placed([P, J], U32, "both2", 2048)))
+        prepare(1)
+        part(runs[2], placed([P, PASSES, 2 * J], U8, "apart2", 4096)[:], gathered[2])
+        iw_cols = placed([P, G * TILES], F32, "iw_cols", 6144)
         nc.scalar.copy(out=iw_cols[:], in_=iw_turned[:, IW_ROW:P])
-        for b, width in enumerate((512, 512, 512)):
-            idle = bank(b, f"idle{b}")
-            nc.tensor.matmul_mx(
-                out=idle[:, 0:width],
-                lhsT=w_codes[0, 0][:, 0:P].bitcast(FP8X4),
-                lhsT_scale=w_scales[0, 0][:, 0:P],
-                rhs=gathered[0][:].bitcast(U8)[:, 0 : 2 * width].bitcast(FP4X4),
-                rhs_scale=picked_scales[:, 0:width],
-                start=True,
-                stop=True,
-            )
-        both2 = look_up(runs[2], placed([P, J], U32, "both2", 0))
+
         late_w = sbuf([P, WIDTH, PACK], BF16, "late_w")
         late_codes = sbuf([P, WIDTH], U32, "late_codes")
         late_scales = sbuf([P, WIDTH], U8, "late_scales")
         for a in range(PASSES):
-            cast(late_w[:, halves[a], :], w_raw[a, 1][:])
             w_codes[a, 1], w_scales[a, 1] = late_codes[:, halves[a]], late_scales[:, halves[a]]
-            quantize(late_w[:, halves[a], :], w_codes[a, 1], w_scales[a, 1])
-            if a == 0:
-                late_apart = sbuf([P, PASSES, 2 * J], U8, "late_apart", "w01_raw")
-                part(runs[2], late_apart[:], both2)
+        cast(late_w[:, halves[0], :], w_raw[0, 1][:])
+        quantize(late_w[:, halves[0], :], w_codes[0, 1], w_scales[0, 1])
+        quarters = [slice(HALF, HALF + P), slice(HALF + P, WIDTH)]
+        cast(late_w[:, quarters[1], :], w_raw[1, 1][:, :, P:HALF], on_vector=True)
+        cast(late_w[:, quarters[0], :], w_raw[1, 1][:, :, 0:P])
+        for cols in quarters:
+            quantize(late_w[:, cols, :], late_codes[:, cols], late_scales[:, cols])
 
-        tab_scale_bytes = tab_scale[:].bitcast(U8)
+        tab_scale_bytes = [t[:].bitcast(U8) for t in tab_scale]
 
-        def look_up_passes(banks, g, h, a):
+        def look_up_passes(banks, g, h, a, opens=0):
             for jt in range(TILES):
                 nc.tensor.matmul_mx(
                     out=banks[jt // 2][:, halves[jt % 2]],
                     lhsT=picked[TILES * g + jt][:, a, :].bitcast(FP4X4),
-                    lhsT_scale=tab_scale_bytes[:, a, g * J + P * jt : g * J + P * (jt + 1)],
+                    lhsT_scale=tab_scale_bytes[a][:, g * J + P * jt : g * J + P * (jt + 1)],
                     rhs=w_codes[a, h].bitcast(FP8X4),
                     rhs_scale=w_scales[a, h],
-                    start=(a == 0 and jt % 2 == 0),
-                    stop=(a == PASSES - 1 and jt % 2 == 1),
+                    start=(a == opens and jt % 2 == 0),
+                    stop=(a != opens and jt % 2 == 1),
                 )
 
         def pair(first, name):
@@ -231,10 +225,10 @@ def tile_list_interp_none_kernel(
         def weigh_and_add(total, so_far, banks, g):
             for jt in range(TILES):
                 nc.vector.scalar_tensor_tensor(
-                    out=total[:, jt, :],
+                    out=total[jt],
                     in0=banks[jt // 2][:, halves[jt % 2]],
                     scalar=weight(g, jt),
-                    in1=so_far[:, jt, :],
+                    in1=so_far[jt],
                     op0=MULT,
                     op1=ADD,
                 )
@@ -244,25 +238,28 @@ def tile_list_interp_none_kernel(
                 for jt in range(TILES):
                     nc.tensor.matmul(
                         banks[t][:, P * jt : P * (jt + 1)],
-                        total[:, jt, P * t : P * (t + 1)],
+                        total[jt][:, P * t : P * (t + 1)],
                         ident[:],
                         is_transpose=True,
                         start=(jt == 0),
                         stop=(jt == TILES - 1),
                     )
 
+        def by_tile(t, count=TILES):
+            return [t[:, jt, :] for jt in range(count)]
+
         sums = {(g, 0): pair(2 * g, f"sum{g}0") for g in range(G)}
         for a in range(PASSES):
             for g in range(G - 1):
                 look_up_passes(sums[g, 0], g, 0, a)
-        for a in range(PASSES):
-            look_up_passes(sums[2, 0], 2, 0, a)
+        for a in reversed(range(PASSES)):
+            look_up_passes(sums[2, 0], 2, 0, a, opens=1)
         terms_a = sbuf([P, TILES, HALF], F32, "terms_a", "w11_raw")
         weigh(terms_a[:], sums[0, 0], 0)
         two_a = sbuf([P, TILES, HALF], F32, "two_a")
-        weigh_and_add(two_a[:], terms_a[:], sums[1, 0], 1)
+        weigh_and_add(by_tile(two_a), by_tile(terms_a), sums[1, 0], 1)
         three_a = sbuf([P, TILES, HALF], F32, "three_a")
-        weigh_and_add(three_a[:], two_a[:], sums[2, 0], 2)
+        weigh_and_add(by_tile(three_a), by_tile(two_a), sums[2, 0], 2)
 
         x0_bf16 = sbuf([P, WIDTH, PACK], BF16, "x0_bf16", "late_w")
         x_codes = [sbuf([P, WIDTH], U32, f"x{a}_codes") for a in range(PASSES)]
@@ -278,30 +275,30 @@ def tile_list_interp_none_kernel(
         terms_b = sbuf([P, TILES, HALF], F32, "terms_b", "x0_raw")
         weigh(terms_b[:], sums[0, 1], 0)
         two_b = sbuf([P, TILES, HALF], F32, "two_b")
-        weigh_and_add(two_b[:], terms_b[:], sums[1, 1], 1)
+        weigh_and_add(by_tile(two_b), by_tile(terms_b), sums[1, 1], 1)
 
         x1_bf16 = sbuf([P, WIDTH, PACK], BF16, "x1_bf16", "late_w")
         cast_on_gpsimd(x1_bf16[:, halves[0], :], x1_raw[:, :, halves[0]])
         cast(x1_bf16[:, halves[1], :], x1_raw[:, :, halves[1]])
         quantize(x1_bf16[:], x_codes[1][:], x_scales[1][:])
-        late = placed([P, 2, TILES, HALF], F32, "late", 8192)
-        three_b = late[:, 0]
-        weigh_and_add(three_b, two_b[:], sums[2, 1], 2)
+        late = placed([P, 3, 2, HALF], F32, "late", 12288)
+        three_b = by_tile(sbuf([P, 2, HALF], F32, "three_b"), 2) + by_tile(late[:, 2], 2)
+        weigh_and_add(three_b, by_tile(two_b), sums[2, 1], 2)
 
         turned_a = pair(4, "turned_a")
-        turn(turned_a, three_a[:])
+        turn(turned_a, by_tile(three_a))
         held = []
         for t in range(2):
-            held.append(late[:, 1, 2 * t : 2 * t + 2, :].rearrange("p c j -> p (c j)"))
+            held.append(late[:, t].rearrange("p c j -> p (c j)"))
             nc.scalar.copy(out=held[t], in_=turned_a[t][:])
 
         wx_scale_bytes = wx_scale[:].bitcast(U8)
         dense = pair(6, "dense_a") + pair(0, "dense_b")
-        for nt in (0, 2, 3, 1):
-            for a in range(PASSES):
+        for a in range(PASSES):
+            for nt in (0, 2, 3, 1):
                 nc.tensor.matmul_mx(
                     out=dense[nt][:],
-                    lhsT=wx_word[:, a, P * nt : P * (nt + 1)].bitcast(FP8X4),
+                    lhsT=wx_word[a][:, P * nt : P * (nt + 1)].bitcast(FP8X4),
                     lhsT_scale=wx_scale_bytes[:, a, P * nt : P * (nt + 1)],
                     rhs=x_codes[a][:].bitcast(FP8X4),
                     rhs_scale=x_scales[a][:],

@@ -78,17 +78,17 @@ def tile_list_interp_none_kernel(
             nc.sync.dma_start(out=raw[:], in_=rows.rearrange("(p i) c -> p i c", i=PACK))
             return raw
 
+        for g, vec in enumerate((iw0, iw1, iw2)):
+            nc.scalar.dma_start(
+                out=iw_rows[IW_ROW + TILES * g : IW_ROW + TILES * (g + 1), :],
+                in_=vec.rearrange("(c p) -> c p", p=P),
+            )
         offsets = lists.tile([P, G * LIST_COLUMNS], U16, name="offsets")
         nc.sync.dma_start(offsets[:], offs)
         nc.sync.dma_start(
             out=scale_window[FIRST_ROW:P, :],
             in_=tab_scales.bitcast(I32).rearrange("a s t -> (a s) t"),
         )
-        for g, vec in enumerate((iw0, iw1, iw2)):
-            nc.gpsimd.dma_start(
-                out=iw_rows[IW_ROW + TILES * g : IW_ROW + TILES * (g + 1), :],
-                in_=vec.rearrange("(c p) -> c p", p=P),
-            )
         word_window = sbuf([P, T], I32, "word_window")
         nc.sync.dma_start(
             out=word_window[:], in_=tab_words[0].rearrange("p t b -> p (t b)").bitcast(I32)
@@ -161,23 +161,38 @@ def tile_list_interp_none_kernel(
         nc.tensor.transpose(iw_turned[:, 0:P], iw_rows[:], ident[:])
 
         w_codes, w_scales = {}, {}
-        runs = [range(TILES * g, TILES * (g + 1)) for g in range(G)]
-
-        def prepare(a):
-            rounded = sbuf([P, HALF, PACK], BF16, f"w{a}0_bf16")
-            cast(rounded[:], w_raw[a, 0][:])
+        for a in range(PASSES):
             w_codes[a, 0] = sbuf([P, HALF], U32, f"w{a}0_codes")[:]
             w_scales[a, 0] = sbuf([P, HALF], U8, f"w{a}0_scales")[:]
-            quantize(rounded[:], w_codes[a, 0], w_scales[a, 0])
 
-        gathered = [look_up(runs[g], sbuf([P, J], U32, f"both{g}")) for g in range(G - 1)]
+        def prepare(a, cols, rounded):
+            cast(rounded[:], w_raw[a, 0][:, :, cols])
+            quantize(rounded[:], w_codes[a, 0][:, cols], w_scales[a, 0][:, cols])
+
+        def words(run, offset=None):
+            name = f"both{run.start}"
+            if offset is None:
+                return look_up(run, sbuf([P, P * len(run)], U32, name))
+            return look_up(run, placed([P, P * len(run)], U32, name, offset))
+
+        def apart(run, offset):
+            return placed([P, PASSES, 2 * P * len(run)], U8, f"apart{run.start}", offset)[:]
+
+        early = [slice(0, P), slice(P, HALF)]
+        runs = [range(0, 4), range(4, 6), range(6, 8), range(8, 10), range(10, 12)]
+        gathered = [words(runs[0]), words(runs[1])]
         part(runs[0], sbuf([P, PASSES, 2 * J], U8, "apart0")[:], gathered[0])
-        prepare(0)
-        part(runs[1], placed([P, PASSES, 2 * J], U8, "apart1", 0)[:], gathered[1])
-        gathered.append(look_up(runs[2], placed([P, J], U32, "both2", 2048)))
-        prepare(1)
-        part(runs[2], placed([P, PASSES, 2 * J], U8, "apart2", 4096)[:], gathered[2])
-        iw_cols = placed([P, G * TILES], F32, "iw_cols", 6144)
+        prepare(0, early[0], placed([P, P, PACK], BF16, "w000_bf16", 20480))
+        gathered.append(words(runs[2], 20480))
+        prepare(0, early[1], sbuf([P, P, PACK], BF16, "w001_bf16"))
+        part(runs[1], apart(runs[1], 0), gathered[1])
+        part(runs[2], apart(runs[2], 1024), gathered[2])
+        gathered.append(words(runs[3], 2048))
+        prepare(1, halves[0], sbuf([P, HALF, PACK], BF16, "w10_bf16"))
+        gathered.append(words(runs[4], 4096))
+        part(runs[3], apart(runs[3], 5120), gathered[3])
+        part(runs[4], apart(runs[4], 6144), gathered[4])
+        iw_cols = placed([P, G * TILES], F32, "iw_cols", 7168)
         nc.scalar.copy(out=iw_cols[:], in_=iw_turned[:, IW_ROW:P])
 
         late_w = sbuf([P, WIDTH, PACK], BF16, "late_w")
@@ -195,15 +210,15 @@ def tile_list_interp_none_kernel(
 
         tab_scale_bytes = [t[:].bitcast(U8) for t in tab_scale]
 
-        def look_up_passes(banks, g, h, a, opens=0):
+        def look_up_passes(banks, g, h, a, opens=0, cols=halves[0]):
             for jt in range(TILES):
                 nc.tensor.matmul_mx(
-                    out=banks[jt // 2][:, halves[jt % 2]],
+                    out=banks[jt // 2][:, halves[jt % 2]][:, cols],
                     lhsT=picked[TILES * g + jt][:, a, :].bitcast(FP4X4),
                     lhsT_scale=tab_scale_bytes[a][:, g * J + P * jt : g * J + P * (jt + 1)],
-                    rhs=w_codes[a, h].bitcast(FP8X4),
-                    rhs_scale=w_scales[a, h],
-                    start=(a == opens and jt % 2 == 0),
+                    rhs=w_codes[a, h][:, cols].bitcast(FP8X4),
+                    rhs_scale=w_scales[a, h][:, cols],
+                    start=(a == opens and jt % 2 == 0 and cols.start == 0),
                     stop=(a != opens and jt % 2 == 1),
                 )
 
@@ -249,9 +264,11 @@ def tile_list_interp_none_kernel(
             return [t[:, jt, :] for jt in range(count)]
 
         sums = {(g, 0): pair(2 * g, f"sum{g}0") for g in range(G)}
-        for a in range(PASSES):
-            for g in range(G - 1):
-                look_up_passes(sums[g, 0], g, 0, a)
+        for cols in early:
+            look_up_passes(sums[0, 0], 0, 0, 0, cols=cols)
+        look_up_passes(sums[1, 0], 1, 0, 0)
+        for g in range(G - 1):
+            look_up_passes(sums[g, 0], g, 0, 1)
         for a in reversed(range(PASSES)):
             look_up_passes(sums[2, 0], 2, 0, a, opens=1)
         terms_a = sbuf([P, TILES, HALF], F32, "terms_a", "w11_raw")

from contextlib import ExitStack

import concourse.mybir as mybir
from concourse.masks import make_identity

K, L, N, T, J = 1024, 1024, 512, 4096, 512
G = 3
FLOPS = 2 * (G * K + L) * N * J

F32 = mybir.dt.float32
BF16 = mybir.dt.bfloat16
I32 = mybir.dt.int32
U32 = mybir.dt.uint32
U16 = mybir.dt.uint16
U8 = mybir.dt.uint8
FP8X4 = mybir.dt.float8_e4m3fn_x4
FP4X4 = mybir.dt.float4_e2m1fn_x4
COPY = mybir.ActivationFunctionType.Copy
MULT = mybir.AluOpType.mult
ADD = mybir.AluOpType.add

P = 128
QUAD = 32
QUADS = P // QUAD
PACK = 4
K_PASS = P * PACK
PASSES = 2
WIDTH = 512
HALVES = 2
HALF = WIDTH // HALVES
TILES = 4
ROWS_A_QUAD = 4
FIRST_ROW = P - QUAD
IW_ROW = P - G * TILES
LIST_COLUMNS = J // 16


def tile_list_interp_none_kernel(
    tc, tab_words, tab_scales, w, x, wx_words, wx_scales, iw0, iw1, iw2, offs, out
):
    nc = tc.nc
    with ExitStack() as ctx:
        lists = ctx.enter_context(tc.tile_pool(name="lists", bufs=1))
        keep = ctx.enter_context(tc.tile_pool(name="keep", bufs=1))
        shared = ctx.enter_context(tc.tile_pool(name="shared", bufs=1))
        psum = ctx.enter_context(tc.psum_pool(name="psum", bufs=1))

        def sbuf(shape, dtype, name, tag=None):
            return keep.tile(shape, dtype, name=name, tag=tag or name, align_bytes=64)

        def placed(shape, dtype, name, offset):
            return shared.tile(shape, dtype, name=name, offset=offset, align_bytes=64)

        def bank(b, name):
            return psum.tile([P, N], F32, name=name, tag=f"bank{b}")

        scale_window = sbuf([P, T // 4], I32, "scale_window")
        nc.vector.memset(scale_window[0:FIRST_ROW, :], 0)
        iw_rows = sbuf([P, P], F32, "iw_rows")
        nc.gpsimd.memset(iw_rows[0:FIRST_ROW, :], 0.0)
        nc.gpsimd.memset(iw_rows[FIRST_ROW:IW_ROW, :], 0.0)
        tab_scale = [sbuf([P, G * J // 4], I32, f"tab_scale{a}") for a in range(PASSES)]
        for a in range(PASSES):
            nc.vector.memset(tab_scale[a][:], 0)
        wx_scale = sbuf([P, PASSES, N // 4], I32, "wx_scale")
        nc.vector.memset(wx_scale[:], 0)
        ident = sbuf([P, P], F32, "ident")
        make_identity(nc, ident[:])

        halves = [slice(0, HALF), slice(HALF, WIDTH)]

        def load(src, a, cols, name, offset=None):
            if offset is None:
                raw = sbuf([P, PACK, cols.stop - cols.start], F32, name)
            else:
                raw = placed([P, PACK, cols.stop - cols.start], F32, name, offset)
            rows = src[a * K_PASS : (a + 1) * K_PASS, cols]
            nc.sync.dma_start(out=raw[:], in_=rows.rearrange("(p i) c -> p i c", i=PACK))
            return raw

        for g, vec in enumerate((iw0, iw1, iw2)):
            nc.scalar.dma_start(
                out=iw_rows[IW_ROW + TILES * g : IW_ROW + TILES * (g + 1), :],
                in_=vec.rearrange("(c p) -> c p", p=P),
            )
        offsets = lists.tile([P, G * LIST_COLUMNS], U16, name="offsets")
        nc.sync.dma_start(offsets[:], offs)
        nc.sync.dma_start(
            out=scale_window[FIRST_ROW:P, :],
            in_=tab_scales.bitcast(I32).rearrange("a s t -> (a s) t"),
        )
        word_window = sbuf([P, T], I32, "word_window")
        nc.sync.dma_start(
            out=word_window[:], in_=tab_words[0].rearrange("p t b -> p (t b)").bitcast(I32)
        )
        picked_scales = sbuf([P, G * J], U8, "picked_scales")
        nc.vector.tensor_copy(picked_scales[:], scale_window[:].bitcast(U8).indirect(offsets[:]))

        def place_scales(a):
            first = FIRST_ROW + a * QUADS * ROWS_A_QUAD
            for r in range(ROWS_A_QUAD):
                rows = slice(first + r, first + QUADS * ROWS_A_QUAD, ROWS_A_QUAD)
                nc.sync.dma_start(
                    out=tab_scale[a][r:P:QUAD, :], in_=picked_scales[rows, :].bitcast(I32)
                )

        w_raw = {}
        for a in range(PASSES):
            w_raw[a, 0] = load(w, a, halves[0], f"w{a}0_raw", 4096 * a)
            place_scales(a)
        for a in range(PASSES):
            w_raw[a, 1] = load(w, a, halves[1], f"w{a}1_raw")
        whole = slice(0, WIDTH)
        x0_raw = load(x, 0, whole, "x0_raw")
        x1_raw = load(x, 1, whole, "x1_raw", 8192)
        wx_scale_rows = wx_scales.bitcast(I32).rearrange("a (q r) n -> r q a n", r=ROWS_A_QUAD)
        for r in range(ROWS_A_QUAD):
            nc.sync.dma_start(out=wx_scale[r:P:QUAD, :, :], in_=wx_scale_rows[r])
        wx_word = [sbuf([P, N], I32, f"wx_word{a}") for a in range(PASSES)]
        for a in range(PASSES):
            nc.sync.dma_start(
                out=wx_word[a][:], in_=wx_words[a].rearrange("p n b -> p (n b)").bitcast(I32)
            )

        def cast(grouped, raw, on_vector=False):
            target = grouped.rearrange("p (c u) i -> p c i u", u=4)
            source = raw.rearrange("p i (c u) -> p c i u", u=4)
            if on_vector:
                nc.vector.tensor_copy(out=target, in_=source)
            else:
                nc.scalar.activation(out=target, in_=source, func=COPY)

        def cast_on_gpsimd(grouped, raw):
            nc.gpsimd.tensor_scalar(
                grouped, raw.rearrange("p i c -> p c i"), 1.0, 0.0, op0=MULT, op1=ADD
            )

        def quantize(grouped, codes, scales):
            nc.vector.quantize_mx(
                out=codes.bitcast(FP8X4),
                scales=scales,
                in_=grouped.rearrange("p c i -> p (c i)"),
            )

        def look_up(run, both):
            entries = offsets[:, run.start * P // 16 : run.stop * P // 16]
            nc.vector.tensor_copy(both[:], word_window[:].bitcast(U32).indirect(entries))
            return both

        picked = {}

        def part(run, apart, both):
            nc.vector.tensor_copy(
                out=apart.bitcast(U16),
                in_=both[:].bitcast(U16).rearrange("p (j a) -> p a j", a=PASSES),
            )
            for m in run:
                picked[m] = apart[:, :, 2 * P * (m - run.start) : 2 * P * (m - run.start + 1)]

        iw_turned = bank(7, "iw_turned")
        nc.tensor.transpose(iw_turned[:, 0:P], iw_rows[:], ident[:])

        w_codes, w_scales = {}, {}
        for a in range(PASSES):
            w_codes[a, 0] = sbuf([P, HALF], U32, f"w{a}0_codes")[:]
            w_scales[a, 0] = sbuf([P, HALF], U8, f"w{a}0_scales")[:]

        def prepare(a, cols, rounded):
            cast(rounded[:], w_raw[a, 0][:, :, cols])
            quantize(rounded[:], w_codes[a, 0][:, cols], w_scales[a, 0][:, cols])

        def words(run, offset=None):
            name = f"both{run.start}"
            if offset is None:
                return look_up(run, sbuf([P, P * len(run)], U32, name))
            return look_up(run, placed([P, P * len(run)], U32, name, offset))

        def apart(run, offset):
            return placed([P, PASSES, 2 * P * len(run)], U8, f"apart{run.start}", offset)[:]

        early = [slice(0, P), slice(P, HALF)]
        runs = [range(0, 4), range(4, 6), range(6, 8), range(8, 10), range(10, 12)]
        gathered = [words(runs[0]), words(runs[1])]
        part(runs[0], sbuf([P, PASSES, 2 * J], U8, "apart0")[:], gathered[0])
        prepare(0, early[0], placed([P, P, PACK], BF16, "w000_bf16", 20480))
        gathered.append(words(runs[2], 20480))
        prepare(0, early[1], sbuf([P, P, PACK], BF16, "w001_bf16"))
        part(runs[1], apart(runs[1], 0), gathered[1])
        part(runs[2], apart(runs[2], 1024), gathered[2])
        gathered.append(words(runs[3], 2048))
        prepare(1, halves[0], sbuf([P, HALF, PACK], BF16, "w10_bf16"))
        gathered.append(words(runs[4], 4096))
        part(runs[3], apart(runs[3], 5120), gathered[3])
        part(runs[4], apart(runs[4], 6144), gathered[4])
        iw_cols = placed([P, G * TILES], F32, "iw_cols", 7168)
        nc.scalar.copy(out=iw_cols[:], in_=iw_turned[:, IW_ROW:P])

        late_w = sbuf([P, WIDTH, PACK], BF16, "late_w")
        late_codes = sbuf([P, WIDTH], U32, "late_codes")
        late_scales = sbuf([P, WIDTH], U8, "late_scales")
        for a in range(PASSES):
            w_codes[a, 1], w_scales[a, 1] = late_codes[:, halves[a]], late_scales[:, halves[a]]
        cast(late_w[:, halves[0], :], w_raw[0, 1][:])
        quantize(late_w[:, halves[0], :], w_codes[0, 1], w_scales[0, 1])
        quarters = [slice(HALF, HALF + P), slice(HALF + P, WIDTH)]
        cast(late_w[:, quarters[1], :], w_raw[1, 1][:, :, P:HALF], on_vector=True)
        cast(late_w[:, quarters[0], :], w_raw[1, 1][:, :, 0:P])
        for cols in quarters:
            quantize(late_w[:, cols, :], late_codes[:, cols], late_scales[:, cols])

        tab_scale_bytes = [t[:].bitcast(U8) for t in tab_scale]

        def look_up_passes(banks, g, h, a, opens=0, cols=halves[0]):
            for jt in range(TILES):
                nc.tensor.matmul_mx(
                    out=banks[jt // 2][:, halves[jt % 2]][:, cols],
                    lhsT=picked[TILES * g + jt][:, a, :].bitcast(FP4X4),
                    lhsT_scale=tab_scale_bytes[a][:, g * J + P * jt : g * J + P * (jt + 1)],
                    rhs=w_codes[a, h][:, cols].bitcast(FP8X4),
                    rhs_scale=w_scales[a, h][:, cols],
                    start=(a == opens and jt % 2 == 0 and cols.start == 0),
                    stop=(a != opens and jt % 2 == 1),
                )

        def pair(first, name):
            return [bank(first + u, f"{name}_{u}") for u in range(2)]

        def weight(g, jt):
            return iw_cols[:, TILES * g + jt : TILES * g + jt + 1]

        def weigh(terms, banks, g):
            for jt in range(TILES):
                nc.scalar.activation(
                    out=terms[:, jt, :],
                    in_=banks[jt // 2][:, halves[jt % 2]],
                    func=COPY,
                    scale=weight(g, jt),
                )

        def weigh_and_add(total, so_far, banks, g):
            for jt in range(TILES):
                nc.vector.scalar_tensor_tensor(
                    out=total[jt],
                    in0=banks[jt // 2][:, halves[jt % 2]],
                    scalar=weight(g, jt),
                    in1=so_far[jt],
                    op0=MULT,
                    op1=ADD,
                )

        def turn(banks, total):
            for t in range(2):
                for jt in range(TILES):
                    nc.tensor.matmul(
                        banks[t][:, P * jt : P * (jt + 1)],
                        total[jt][:, P * t : P * (t + 1)],
                        ident[:],
                        is_transpose=True,
                        start=(jt == 0),
                        stop=(jt == TILES - 1),
                    )

        def by_tile(t, count=TILES):
            return [t[:, jt, :] for jt in range(count)]

        sums = {(g, 0): pair(2 * g, f"sum{g}0") for g in range(G)}
        for cols in early:
            look_up_passes(sums[0, 0], 0, 0, 0, cols=cols)
        look_up_passes(sums[1, 0], 1, 0, 0)
        for g in range(G - 1):
            look_up_passes(sums[g, 0], g, 0, 1)
        for a in reversed(range(PASSES)):
            look_up_passes(sums[2, 0], 2, 0, a, opens=1)
        terms_a = sbuf([P, TILES, HALF], F32, "terms_a", "w11_raw")
        weigh(terms_a[:], sums[0, 0], 0)
        two_a = sbuf([P, TILES, HALF], F32, "two_a")
        weigh_and_add(by_tile(two_a), by_tile(terms_a), sums[1, 0], 1)
        three_a = sbuf([P, TILES, HALF], F32, "three_a")
        weigh_and_add(by_tile(three_a), by_tile(two_a), sums[2, 0], 2)

        x0_bf16 = sbuf([P, WIDTH, PACK], BF16, "x0_bf16", "late_w")
        x_codes = [sbuf([P, WIDTH], U32, f"x{a}_codes") for a in range(PASSES)]
        x_scales = [sbuf([P, WIDTH], U8, f"x{a}_scales") for a in range(PASSES)]
        cast_on_gpsimd(x0_bf16[:, halves[0], :], x0_raw[:, :, halves[0]])
        cast(x0_bf16[:, halves[1], :], x0_raw[:, :, halves[1]])
        quantize(x0_bf16[:], x_codes[0][:], x_scales[0][:])

        for g, first in enumerate((6, 0, 2)):
            sums[g, 1] = pair(first, f"sum{g}1")
            for a in range(PASSES):
                look_up_passes(sums[g, 1], g, 1, a)
        terms_b = sbuf([P, TILES, HALF], F32, "terms_b", "x0_raw")
        weigh(terms_b[:], sums[0, 1], 0)
        two_b = sbuf([P, TILES, HALF], F32, "two_b")
        weigh_and_add(by_tile(two_b), by_tile(terms_b), sums[1, 1], 1)

        x1_bf16 = sbuf([P, WIDTH, PACK], BF16, "x1_bf16", "late_w")
        cast_on_gpsimd(x1_bf16[:, halves[0], :], x1_raw[:, :, halves[0]])
        cast(x1_bf16[:, halves[1], :], x1_raw[:, :, halves[1]])
        quantize(x1_bf16[:], x_codes[1][:], x_scales[1][:])
        late = placed([P, 3, 2, HALF], F32, "late", 12288)
        three_b = by_tile(sbuf([P, 2, HALF], F32, "three_b"), 2) + by_tile(late[:, 2], 2)
        weigh_and_add(three_b, by_tile(two_b), sums[2, 1], 2)

        turned_a = pair(4, "turned_a")
        turn(turned_a, by_tile(three_a))
        held = []
        for t in range(2):
            held.append(late[:, t].rearrange("p c j -> p (c j)"))
            nc.scalar.copy(out=held[t], in_=turned_a[t][:])

        wx_scale_bytes = wx_scale[:].bitcast(U8)
        dense = pair(6, "dense_a") + pair(0, "dense_b")
        for a in range(PASSES):
            for nt in (0, 2, 3, 1):
                nc.tensor.matmul_mx(
                    out=dense[nt][:],
                    lhsT=wx_word[a][:, P * nt : P * (nt + 1)].bitcast(FP8X4),
                    lhsT_scale=wx_scale_bytes[:, a, P * nt : P * (nt + 1)],
                    rhs=x_codes[a][:].bitcast(FP8X4),
                    rhs_scale=x_scales[a][:],
                    start=(a == 0),
                    stop=(a == PASSES - 1),
                )
        for nt in range(2, TILES):
            copied = sbuf([P, J], F32, f"dense{nt}")
            nc.scalar.copy(out=copied[:], in_=dense[nt][:])
            held.append(copied[:])
        turned_b = pair(0, "turned_b")
        turn(turned_b, three_b)

        for nt, last in enumerate(dense[0:2] + turned_b):
            result = sbuf([P, J], F32, f"result{nt}")
            nc.vector.tensor_tensor(out=result[:], in0=last[:], in1=held[nt], op=ADD)
            nc.sync.dma_start(out=out[P * nt : P * (nt + 1), :], in_=result[:])
